import numpy as np, ml_dtypes
CORES = [5,29,101,125,133,157,229,253]
N = 8
BF = ml_dtypes.bfloat16
def gentries(a):
    return np.ascontiguousarray(a.reshape(8, 16, -1).transpose(0, 2, 1)).reshape(8, -1)
def gtable(e):
    e = np.asarray(e); return np.ascontiguousarray(e.reshape(8, -1, 16).transpose(0, 2, 1)).reshape(128, -1).astype(np.int32)
C, L, HOPS = 2048, 2, (1, 3, 1, 3, 1, 3)
W = C * L; RO = len(HOPS); B = 2 ** RO; NB = C // B
def lay(rng):
    P = np.argsort(rng.random((8, W)), axis=-1)
    for g in range(8):
        for k, v in ((W - 1, W - 1), (W - 2, 0)):
            j = int(np.flatnonzero(P[g] == v)[0]); P[g, j] = P[g, k]; P[g, k] = v
    return P.reshape(8, NB, B, L)
def turned(rng, P):
    ix = (np.arange(L) + rng.integers(0, L, (N, NB, B))[..., None]) % L
    return np.array(np.take_along_axis(np.broadcast_to(P, (N,) + P.shape), np.broadcast_to(ix[:, None], (N,) + P.shape), -1))
def mix(rng, e, b):
    for q in range(N):
        for g in range(8): e[q, g, b] = rng.permutation(e[q, g, b].reshape(-1)).reshape(B, L)
def pack(e, x):
    return {"o": np.stack([gtable(a) for a in e.reshape(N, 8, W)]), "x": np.ascontiguousarray(x.reshape(N, 128, W)).astype(np.float32).astype(BF)}
def place(P, v):
    inv = np.argsort(P.reshape(8, W), axis=-1)
    return np.take_along_axis(v.reshape(N, 8, 16, W), np.broadcast_to(inv[None, :, None, :], (N, 8, 16, W)), -1)
def parity():
    return np.array([bin(i).count("1") % 2 for i in range(B)])
def setup_inputs(rng):
    return pack(np.argsort(rng.random((N, 8, W)), axis=-1), rng.integers(0, 16, (N, 8, 16, W)))
def setup_inputs_spread(rng):
    hi = rng.integers(1, 17, (N, 8, 1, W)) * (rng.random((N, 8, 1, W)) > 0.0625)
    v = np.floor(hi * rng.random((N, 8, 16, W)) ** rng.choice(np.array([0.5, 1.0, 2.0, 4.0]), (N, 8, 16, 1)))
    return pack(np.argsort(rng.random((N, 8, W)), axis=-1), v)
def setup_inputs_ends(rng):
    P = lay(rng); e = turned(rng, P); v = 15 * rng.integers(0, 2, (N, 8, 16, NB, B, L)); flip = rng.integers(0, 2, (N, 1, 1, 1, 1)); par = parity()[:, None]
    for b in range(NB):
        k = (NB - 1 - b) % 4
        if k == 2: mix(rng, e, b); continue
        v[:, :, :, b] = 15 * ((par if k != 1 else 0 * par) ^ flip)
        if k < 2: v[:, 7, 15, b] = np.where(rng.random((N, B, L)) < 0.5, 15 - v[:, 7, 15, b], v[:, 7, 15, b])
    return pack(e, place(P, v))
def setup_inputs_edge(rng):
    P = lay(rng); e = turned(rng, P); v = rng.integers(0, 2, (N, 8, 16, NB, B, L)); flip = rng.integers(0, 2, (N, 1, 1, 1, 1)); par = parity()[:, None]
    for b in range(NB):
        k = (NB - 1 - b) % 4
        if k == 0:
            v[:, :, :, b] = 15 * (par ^ flip); v[:, 7, 15, b] = rng.integers(7, 10, (N, B, L))
        if k == 1:
            h = rng.integers(0, 15, (N, 8, 16, 1, L // 2)); v[:, :, :, b] = h[..., np.arange(L) % (L // 2)]
            v[:, 0, 0, b, :, 0] += rng.integers(0, 2, (N, B))
        if k == 2: mix(rng, e, b)
        if k == 3: v[:, :, :, b] = rng.integers(0, 16, (N, 8, 16, B, 1))
    return pack(e, place(P, v))
def setup_inputs_gap(rng):
    P = lay(rng); e = turned(rng, P); v = np.zeros((N, 8, 16, NB, B, L), np.int64); flip = rng.integers(0, 2, (N, 1, 1, 1, 1)); par = parity()[:, None]
    col = np.arange(L)[None, :]; z = int(rng.integers(0, 4))
    for b in range(NB):
        k = (NB - 1 - b) % 4
        if k == 0 or k == 3:
            v[:, :, :, b] = 15 * ((col % 2 if k == 0 else col // (L // 2)) ^ flip)
            v[:, 7, 15, b] = np.abs(v[:, 7, 15, b] - rng.integers(0, 2, (N, B, L)))
        if k == 1:
            for q in range(N):
                fl = int(flip[q, 0, 0, 0, 0]); u = 15 * ((col % 2) ^ (0 * par) ^ fl); w = 15 * ((col % 2) ^ par ^ fl)
                for m in range(8):
                    g = (m + 2 * (q + z)) % 8
                    if m < 3: v[q, g, :, b] = w
                    if m == 3 or m == 6: v[q, g, :, b] = u
                    if m == 4 or m == 5:
                        for i in rng.permutation(16)[:8]: v[q, g, int(i), b] = u
                    if m == 7: v[q, g, :, b] = rng.integers(0, 16, (16, B, 1))
        if k == 2:
            v[:, :, :, b] = 15 * (par ^ flip)
            up = par ^ flip[:, 0, 0]; h = rng.integers(1, 16, (N, 1, 1))
            v[:, 7, 15, b] = np.where(np.arange(L) == rng.integers(0, L, (N, B, 1)), h - up, 15 * up)
    return pack(e, place(P, v))
def setup_inputs_corners(rng):
    one = np.arange(W); e = np.argsort(rng.random((N, 8, W)), axis=-1)
    for g in range(8):
        both = rng.permutation(W)
        for q in range(N):
            h = (g + 2 * (q % 2)) % 8
            if h == 0: e[q, g] = one
            if h == 1: e[q, g] = one[::-1]
            if h == 2: e[q, g] = np.roll(one, 1)
            if h == 3: e[q, g] = both
            if h == 4: e[q, g] = one.reshape(L, C).T.reshape(-1)
            if h == 5: e[q, g] = np.argsort(both)
            if h == 6: e[q, g] = np.roll(one.reshape(C, L), q + 1, axis=1).reshape(-1)
    x = rng.integers(0, 16, (N, 8, 16, W)); w = rng.permutation(N)
    x[w[0]] = 15; x[w[1], :7] = 0; x[w[2], ::2] = 15 * rng.integers(0, 2, (4, 16, W))
    return pack(e, x)
def check_inputs(d):
    bad = []; v = np.asarray(d["x"]).astype(np.float32); c = np.asarray(d["o"])
    if not np.all((v >= 0) & (v <= 15)): bad.append("range of x")
    if not np.all(v == np.floor(v)): bad.append("whole numbers of x")
    if np.min(c) < 0 or np.max(c) > W - 1: bad.append("range of o")
    if np.any(np.sort(np.stack([gentries(a) for a in c]), axis=-1) != np.arange(W)): bad.append("permutation of o")
    return bad
def reference(o, x):
    cy = np.stack([gentries(a) for a in o]).astype(np.int64)
    xv = x.astype(np.float32).astype(np.int32).reshape(N, 8, 16, W); num = np.arange(C)
    for t in range(RO):
        lo = num[(num >> t) % 2 == 0]; hi = lo + 2 ** t; roots = []
        for q in range(N):
            cq = cy[q].reshape(8, C, L); a = cq[:, lo]; b = cq[:, hi]
            xa = np.take_along_axis(xv[q], a.reshape(8, 1, -1), 2).reshape(128, C // 2, L)
            xb = np.take_along_axis(xv[q], b.reshape(8, 1, -1), 2).reshape(128, C // 2, L)
            score = np.stack([np.add.reduce(np.abs(xa - np.roll(xb, -k, axis=2)), axis=(0, 2)) for k in range(L)])
            s = np.argmin(score, axis=0)
            ix = np.broadcast_to((np.arange(L)[None, :] + s[:, None]) % L, b.shape)
            bs = np.take_along_axis(b, ix, 2)
            f = np.zeros((8, W), np.int64)
            np.put_along_axis(f, a.reshape(8, -1), bs.reshape(8, -1), 1)
            np.put_along_axis(f, bs.reshape(8, -1), np.roll(a, -1, axis=2).reshape(8, -1), 1)
            roots.append(f)
        cy = np.stack([np.take_along_axis(roots[(r - HOPS[t]) % N], cy[r], 1) for r in range(N)])
    return {"yo": np.stack([gtable(e) for e in cy]).astype(np.float32)}

@@ -1,0 +1,461 @@
+from concourse.bass import DstId, RemoteDMATransfer
+from concourse.mybir import AluOpType, ActivationFunctionType
+
+HOPS = (1, 3, 1, 3, 1, 3)
+RO = len(HOPS)
+NV = 96
+HV = 120
+GV = 128
+IV = 132
+BV = 32
+PQ = (4, 4, 4, 2, 2)
+NDMA = 60
+
+F, I, U, B = "float32", "int32", "uint16", "bfloat16"
+SCRATCH = {
+    "xs": ("sbuf", [128, 4096], B), "V0": ("sbuf", [128, 4096], F), "V1": ("sbuf", [128, 4096], F),
+    "V2": ("sbuf", [128, 4096], F), "Z": ("sbuf", [128, 4096], F), "GO": ("sbuf", [128, 4096], F),
+    "AB": ("sbuf", [128, 4096], F), "ZD": ("sbuf", [128, 4096], F), "CW": ("sbuf", [128, 4096], F),
+    "M1": ("sbuf", [128, 2048], B), "M2": ("sbuf", [128, 2048], B), "bb": ("sbuf", [128, 2048], B),
+    "G": ("sbuf", [128, 256], I), "G16": ("sbuf", [128, 256], U), "Gr": ("sbuf", [128, 256], F),
+    "Y": ("sbuf", [128, 16, 32], F), "Yt": ("sbuf", [128, 16, 32], F), "zero": ("sbuf", [128, 256], F),
+    "pi": ("sbuf", [128, 1], I), "pj": ("sbuf", [128, 1], I), "pk": ("sbuf", [128, 1], I),
+    "m0": ("sbuf", [128, 1], F), "m1": ("sbuf", [128, 1], F), "pc": ("sbuf", [128, 1], F),
+    "Wp": ("sbuf", [128, 144], B), "Wn": ("sbuf", [128, 144], B),
+    "dg": ("sbuf", [128, 128], F), "Ip": ("sbuf", [128, 128], F), "In": ("sbuf", [128, 128], F),
+    "Jp": ("sbuf", [128, 128], B), "Jn": ("sbuf", [128, 128], B),
+    "c16": ("sbuf", [128, 256], F), "cod": ("sbuf", [128, 256], F),
+    "xb0": ("sbuf", [128, 256], B), "xb1": ("sbuf", [128, 256], B),
+    "st": ("sbuf", [128, 256], F), "emb": ("sbuf", [128, 256], F), "et": ("sbuf", [128, 256], F),
+    "ti": ("sbuf", [128, 256], I), "tk": ("sbuf", [128, 256], I), "tl": ("sbuf", [128, 256], I),
+    "rE": ("sbuf", [128, 256], B), "rL": ("sbuf", [128, 256], B), "rH": ("sbuf", [128, 256], B),
+    "ra": ("sbuf", [128, 128], B), "rb": ("sbuf", [128, 128], B),
+    "H16": ("sbuf", [128, 256], U), "Hs16": ("sbuf", [128, 128], U), "o16": ("sbuf", [128, 256], U),
+    "L16": ("sbuf", [128, 256], U), "Hf": ("sbuf", [128, 256], F),
+    "Ea": ("sbuf", [128, 128], F), "Eb": ("sbuf", [128, 128], F),
+    "da": ("sbuf", [128, 64], F), "db": ("sbuf", [128, 64], F), "ea": ("sbuf", [128, 64], F),
+    "eb": ("sbuf", [128, 64], F), "s": ("sbuf", [128, 64], F),
+    "Tv": ("sbuf", [128, 256], F), "Ta": ("sbuf", [128, 256], F),
+    "D": ("psum", [128, 512], F), "Pa": ("psum", [128, 512], F), "Pb": ("psum", [128, 512], F),
+    "Pe": ("psum", [128, 512], F), "Ps": ("psum", [128, 512], F), "Pl": ("psum", [128, 512], F),
+    "Ph": ("psum", [128, 512], F),
+}
+for _w in range(3):
+    SCRATCH["X%d0" % _w] = ("sbuf", [128, 256], F)
+    SCRATCH["X%d1" % _w] = ("sbuf", [128, 256], F)
+for _t in range(RO):
+    SCRATCH["N%d" % _t] = ("sbuf", [128, 2 ** (6 - _t), 2, 2 ** (_t + 1)], U if _t else F)
+    SCRATCH["B%d" % _t] = ("sbuf", [128, 2 ** (7 - _t), 2, 2 ** _t] if _t else [128, 128, 2], F)
+    SCRATCH["Bout%d" % _t] = ("sbuf", [128, 256], U)
+    SCRATCH["Bin%d" % _t] = ("sbuf", [128, 256], U)
+    SCRATCH["Iin%d" % _t] = ("sbuf", [128, 256], F)
+    if _t:
+        SCRATCH["Iex%d" % _t] = ("sbuf", [128, 256], F)
+
+SEMAPHORES = (["cv", "ca", "cp", "cg", "sent"] + ["d%d" % _i for _i in range(NDMA)]
+              + ["b%d_%d" % (_t, _h) for _t in range(RO) for _h in range(2)] + ["i%d" % _t for _t in range(RO)])
+
+OFF = 192.0
+MID = 2047.5
+LIFT = 32.0
+
+
+def bits(engines):
+    m = 0
+    for e in engines:
+        m |= 1 << e
+    return m
+
+
+def helpers(core, T, topo):
+    r = T.rank_of(core)
+    n = len(T.cores)
+    dsts = [T.cores[(r + h) % n] for h in set(HOPS)]
+    ok = [c for c in topo.cores_of(core) if T.rank_of(c) is None and all(topo.may_write(c, d) for d in dsts)]
+    ok.sort(key=lambda c: (topo.die(c) != topo.die(core), c))
+    return ok[:2]
+
+
+def helper_program(g, core, owner, half, T, topo):
+    r = T.rank_of(owner)
+    n = len(T.cores)
+    got = len(topo.engines(owner, core)) // 2
+    cols = slice(128 * half, 128 * half + 128)
+    total = 0
+    for t in range(RO):
+        dst = T.cores[(r + HOPS[t]) % n]
+        rid, pid = topo.addr(dst, core)
+        for buf, sem in (("Iin%d" % t, "i%d" % t), ("Bin%d" % t, "b%d_%d" % (t, half))):
+            g.wait_ge(T.sem[sem], got)
+            g.remote_dma(T[buf][:, cols], T[buf][:, cols], T.sem[sem], T.sem.sent, pid, rid, topo.mask(core, dst))
+            total += len(topo.engines(core, dst))
+    g.wait_ge(T.sem.sent, total)
+
+
+def rank_program(g, core, T, topo):
+    rank = T.rank_of(core)
+    if rank is None:
+        for owner in topo.cores_of(core):
+            if T.rank_of(owner) is not None:
+                hs = helpers(owner, T, topo)
+                if core in hs:
+                    helper_program(g, core, owner, hs.index(core), T, topo)
+        return
+    n = len(T.cores)
+    A = AluOpType
+    ACT = ActivationFunctionType
+    Q = {"v": g.vector, "a": g.scalar, "p": g.tensor, "g": g, "s": g.sync}
+    seen = {q: {} for q in Q}
+    wr, rd, top = {}, {}, {}
+    ndma = [0]
+
+    def need(q, toks):
+        for sem, val in toks.items():
+            if seen[q].get(sem, 0) < val:
+                Q[q].wait_ge(T.sem[sem], val)
+                seen[q][sem] = val
+
+    def order(q, reads, writes):
+        for k in reads:
+            need(q, wr.get(k, {}))
+        for k in writes:
+            need(q, wr.get(k, {}))
+            need(q, rd.get(k, {}))
+
+    def note(sem, val, reads, writes, also):
+        top[sem] = val
+        for k in reads:
+            rd.setdefault(k, {})[sem] = val
+        for k in writes:
+            wr[k] = {sem: val}
+            rd[k] = {}
+        for k in also:
+            wr[k][sem] = val
+
+    def op(q, call, reads, writes, also=()):
+        order(q, reads, writes)
+        sem = "c" + q
+        call().then_inc(T.sem[sem], 1)
+        note(sem, top.get(sem, 0) + 1, reads, writes, also)
+
+    def batch(q, calls, reads, key):
+        for i, call in enumerate(calls):
+            op(q, call, reads, [] if i else [key], [key] if i else [])
+
+    def dma(out, in_, reads, writes):
+        order("s", reads, writes)
+        sem = "d%d" % ndma[0]
+        ndma[0] += 1
+        g.sync.dma_start(out, in_).then_inc(T.sem[sem], 16)
+        note(sem, 16, reads, writes, ())
+
+    hs = helpers(core, T, topo)
+
+    def send(srcs, land, sems, reads):
+        order("g", reads, [])
+        tr = []
+        for h in range(2):
+            e = topo.engines(core, hs[h])
+            e = e[h * len(e) // 2:(h + 1) * len(e) // 2]
+            rid, pid = topo.addr(hs[h], core)
+            cols = slice(128 * h, 128 * h + 128)
+            to = [DstId(rid=rid, pnc=pid)]
+            if len(srcs) == 1:
+                tr.append(RemoteDMATransfer(dst_ids=to, dma_engine_mask=bits(e), remote_sem=T.sem[sems[h]],
+                                            src=srcs[0][:, cols], dst=land[:, cols]))
+            else:
+                tr.append(RemoteDMATransfer(dst_ids=to, dma_engine_mask=bits(e), remote_sem=T.sem[sems[h]],
+                                            srcs=[x[:, cols] for x in srcs], dsts=[land[:, cols]], alu_op=1))
+            top["sent"] = top.get("sent", 0) + len(e)
+        g.remote_dma_fused(tr, local_sem=T.sem.sent)
+
+    for t in range(RO):
+        src = T.cores[(rank - HOPS[t]) % n]
+        cnt = [len(topo.engines(h, core)) for h in helpers(src, T, topo)]
+        wr["Iin%d" % t] = {"i%d" % t: sum(cnt)}
+        top["i%d" % t] = sum(cnt)
+        for h in range(2):
+            wr["Bin%d_%d" % (t, h)] = {"b%d_%d" % (t, h): cnt[h]}
+            top["b%d_%d" % (t, h)] = cnt[h]
+
+    V, S = g.vector, g.scalar
+
+    def ts(out, in_, s1, s2, o1, o2=None):
+        if o2 is None:
+            return lambda: V.tensor_scalar(out, in_, s1, None, o1)
+        return lambda: V.tensor_scalar(out, in_, s1, s2, o1, o2)
+
+    def cp(out, in_):
+        return lambda: V.tensor_copy(out, in_)
+
+    def tt(out, a, b, o):
+        return lambda: V.tensor_tensor(out, a, b, o)
+
+    def act(out, in_, bias=None):
+        if bias is None:
+            return lambda: S.activation(out, in_, ACT.Identity)
+        return lambda: S.activation(out, in_, ACT.Identity, bias=float(bias))
+
+    def code(out, frac, extra=0.0):
+        return ts(out, frac, 4096.0, MID + extra, A.mult, A.add)
+
+    def gv(out, win, lst, a, b, reads, keys):
+        op("v", cp(out[:, 16 * a:16 * b], win[:].indirect(lst[:, a:b])), reads, keys)
+
+    def ga(out, win, lst, a, b, reads, keys, also=()):
+        op("a", act(out[:, 16 * a:16 * b], win[:].indirect(lst[:, a:b])), reads, keys, also)
+
+    def lin(groups, reads, key):
+        calls = []
+        for out, terms in groups:
+            for i, (W, x) in enumerate(terms):
+                calls.append(lambda out=out, W=W, x=x, a=(i == 0), z=(i == len(terms) - 1): g.tensor.matmul(out, W[:], x, a, z))
+        batch("p", calls, reads + ["ident"], key)
+
+    def role(t, side, j):
+        return T["N%d" % t][:, :, side, j::2] if t else T.N0[:, :, side, j]
+
+    def brole(t, side, j):
+        hi = 2 ** (6 - t)
+        return T["B%d" % t][:, j * hi:(j + 1) * hi, side, :] if t else T.B0[:, j * hi:(j + 1) * hi, side]
+
+    first_mm = [True]
+
+    def sums(items, reads, last):
+        for i, (P, W, rhs) in enumerate(items):
+            st, fin = first_mm[0], last and i == len(items) - 1
+            first_mm[0] = fin
+            op("p", lambda: g.tensor.matmul(T.D[:, 0:64], W[:, 16 - P:144 - P], rhs, st, fin),
+               reads + ["Wp", "Wn"], ["D"] if st else [], [] if st else ["D"])
+
+    ABK = ["ABa0", "ABa1", "ABb0", "ABb1", "ABb2"]
+
+    dma(T.G[:], T.o[:], [], ["G"])
+    op("g", lambda: g.iota(T.ZD[:, 0:256], [[16, 128], [2048, 2]], int(LIFT), 0, allow_small_or_imprecise_dtypes=True),
+       [], ["ZD0"])
+    op("g", lambda: g.iota(T.pi[:], [[1, 1]], 0, 1), [], ["pi"])
+    op("g", lambda: g.iota(T.c16[:], [[16, 256]], 0, 0, allow_small_or_imprecise_dtypes=True), [], ["c16"])
+    op("g", lambda: g.iota(T.dg[:], [[1, 128]], 0, -1, allow_small_or_imprecise_dtypes=True), [], ["dg"])
+    op("g", lambda: g.iota(T.CW[:], [[1, 16], [16, 256]], 0, 0, allow_small_or_imprecise_dtypes=True), [], ["CW"])
+    op("v", lambda: V.memset(T.zero[:], 0.0), [], ["zero"])
+    dma(T.Z[0:128:16, :], T.zero[:], ["zero"], ["Z.v"])
+    dma(T.GO[0:128:16, :], T.zero[:], ["zero"], ["GO.a"])
+    dma(T.xs[:], T.x[:], [], ["xs"])
+    dma(T.xb0[:], T.x[0:128:16, :], [], ["xb0"])
+    dma(T.xb1[:], T.x[1:128:16, :], [], ["xb1"])
+    op("v", lambda: V.memset(T.Wp[:], 0.0), [], ["Wp"])
+    op("v", lambda: V.memset(T.Wn[:], 0.0), [], ["Wn"])
+    nb = NV // 16
+    batch("v", [ts(T.ZD[:, 256 * P:256 * P + 256], T.ZD[:, 0:256], float(P), None, A.add) for P in range(1, nb)],
+          ["ZD0"], "ZDv")
+    batch("a", [act(T.ZD[:, 256 * P:256 * P + 256], T.ZD[:, 0:256], P) for P in range(nb, 16)], ["ZD0"], "ZDa")
+    op("v", lambda: V.memset(T.Wp[:, 0:144:16], 1.0), [], ["Wp"])
+    op("v", lambda: V.memset(T.Wn[:, 0:144:16], -1.0), [], ["Wn"])
+    op("v", ts(T.pj[:], T.pi[:], 4, 1, A.logical_shift_right, A.bitwise_and), ["pi"], ["pj"])
+    op("v", ts(T.pk[:], T.pi[:], 15, None, A.bitwise_and), ["pi"], ["pk"])
+    op("v", cp(T.m1[:], T.pj[:]), ["pj"], ["m1"])
+    op("v", ts(T.m0[:], T.pj[:], -1.0, 1.0, A.mult, A.add), ["pj"], ["m0"])
+    op("v", ts(T.pc[:], T.pk[:], -MID, None, A.add), ["pk"], ["pc"])
+    op("v", cp(T.G16[:], T.G[:]), ["G"], ["G16"])
+    op("a", lambda: S.activation(T.GO[:].indirect(T.G16[:, NV:256]), T.ZD[:, 16 * NV:4096], ACT.Silu),
+       ["G16", "ZDa"], ["GO.a"])
+    op("v", cp(T.Z[:].indirect(T.G16[:, 0:NV]), T.ZD[:, 0:16 * NV]), ["G16", "ZD0", "ZDv"], ["Z.v"])
+    dma(T.Tv[:], T.Z[0:128:16, :], ["Z.v"], ["Tv"])
+    dma(T.Ta[:], T.GO[0:128:16, :], ["GO.a"], ["Ta"])
+    rd["Z.a"], rd["GO.v"] = dict(rd["Z.v"]), dict(rd["GO.a"])
+    send([T.Tv, T.Ta], T.Iin0, ["i0", "i0"], ["Tv", "Ta"])
+    batch("v", [cp(T.Gr[:, 16 * u:16 * u + 16], T.G[:, u:256:16]) for u in range(16)], ["G"], "Gr")
+    batch("v", [ts(T.Y[:, :, 0:16], T.Gr[:], T.m0[:], None, A.mult),
+                ts(T.Y[:, :, 16:32], T.Gr[:], T.m1[:], None, A.mult)], ["Gr", "m0", "m1"], "Y")
+    batch("v", [(lambda u=u: V.transpose(T.Yt[:, u, :], T.Y[:, u, :])) for u in range(16)], ["Y"], "Yt")
+    op("v", tt(T.N0[:], T.Yt[:, :, 0:16], T.Yt[:, :, 16:32], A.add), ["Yt"], ["N"])
+    batch("v", [cp(T.H16[:, 128 * sd + 64 * j:128 * sd + 64 * j + 64], role(0, sd, j)) for sd in (1, 0) for j in (0, 1)],
+          ["N"], "H16")
+    batch("v", [cp(T.Hs16[:, 64 * (1 - j):64 * (1 - j) + 64], role(0, 0, j)) for j in (0, 1)], ["N"], "Hs16")
+
+    def window(w, a=0, b=16):
+        Vw = T["V%d" % w]
+        if w == 0:
+            pairs = [(Vw[:], T.xs[:])]
+        elif w == 1:
+            pairs = [(Vw[:, u:4096:16], T.xs[:, 256 * u:256 * u + 256]) for u in range(16)]
+        else:
+            pairs = [(Vw[:, 256 * u:256 * u + 256], T.xs[:, u:4096:16]) for u in range(16)]
+        for k in range(a, min(b, len(pairs))):
+            op("a", act(pairs[k][0], pairs[k][1], OFF), ["xs"], [] if k else ["V%d" % w], ["V%d" % w] if k else [])
+
+    def rows(w):
+        for p in range(2):
+            dma(T["X%d%d" % (w, p)][:], T["V%d" % w][p:128:16, :], ["V%d" % w], ["X%d%d" % (w, p)])
+
+    def side_codes(E, r, P):
+        op("a", act(T[r][:], T[E][:]), [E], [r])
+        return lambda: lin([(T[P][:, 0:128], [(T.Ip, T[E][:]), (T.Jn, T[r][:])]),
+                            (T[P][:, 128:192], [(T.Ip, T[E][:, 64:128]), (T.In, T[E][:, 0:64]),
+                                                (T.Jn, T[r][:, 64:128]), (T.Jp, T[r][:, 0:64])])], [E, r], P)
+
+    def inverse_row(t):
+        Vn = "V%d" % (t % 3)
+        op("a", act(T.emb[:], T.Pe[:, 0:256]), ["Pe"], ["emb"])
+        dma(T[Vn][1:128:16, :], T.emb[:], ["emb", Vn], [Vn + "i"])
+
+    def place_row(t):
+        Vn = "V%d" % (t % 3)
+        if t < 3:
+            op("a", act(T.st[:], T.Ps[:, 0:256]), ["Ps"], ["st"])
+            dma(T[Vn][0:128:16, :], T.st[:], ["st", Vn], [Vn + "c"])
+
+    zk = ["Z.v", "Z.a"]
+    for t in range(RO + 1):
+        w = (t - 1) % 3
+        X0, X1 = "X%d0" % (t % 3), "X%d1" % (t % 3)
+        if t > 0:
+            win, wk = (T["V%d" % w], ["V%d" % w, "V%dc" % w, "V%di" % w]) if t < RO else (T.CW, ["CW"])
+            b0, b1 = "Bin%d_0" % (t - 1), "Bin%d_1" % (t - 1)
+            Bin = T["Bin%d" % (t - 1)]
+            gv(T.Z, win, Bin, 0, GV, wk + [b0] + ([b1] if GV > 128 else []), ["Z.v"])
+            ga(T.Z, win, Bin, GV, 256, wk + [b1] + ([b0] if GV < 128 else []), ["Z.a"])
+
+            def round_h():
+                op("a", act(T.rH[:], T.Hf[:]), ["Hf"], ["rH"])
+                lin([(T.Ph[:, 0:256], [(T.Ip, T.Hf[:]), (T.Jn, T.rH[:])])], ["Hf", "rH"], "Ph")
+
+            if t == RO:
+                round_h()
+                op("v", code(T.H16[:], T.Ph[:, 0:256]), ["Ph"], ["H16"])
+                gv(T.GO, T.Z, T.H16, 0, 128, zk + ["H16"], ["GO.v"])
+                ga(T.GO, T.Z, T.H16, 128, 256, zk + ["H16"], ["GO.a"])
+                dma(T.yo[:], T.GO[0:128:16, :], ["GO.v", "GO.a"], [])
+                break
+            gv(T.GO, T.Z, T.L16, 0, IV, zk + ["L16"], ["GO.v"])
+            mid = (IV + 256) // 4 * 2
+            ga(T.GO, T.Z, T.L16, IV, mid, zk + ["L16"], ["GO.a"])
+            if t > 1:
+                round_h()
+            ga(T.GO, T.Z, T.L16, mid, 256, zk + ["L16"], [], ["GO.a"])
+            dma(T["Iex%d" % t][:], T.GO[1:128:16, :], ["GO.v", "GO.a"], ["Iex"])
+            send([T["Iex%d" % t]], T["Iin%d" % t], ["i%d" % t] * 2, ["Iex"])
+            if t > 1:
+                hk = "Ph"
+                hl = lambda o, a, b: code(o, T.Ph[:, a:b])
+            else:
+                hk = "Hf"
+                hl = lambda o, a, b: ts(o, T.Hf[:, a:b], 0.25 - LIFT, None, A.add)
+            batch("v", [hl(T.H16[:, r:256:8], 32 * r, 32 * r + 32) for r in range(8)], [hk], "H16")
+            gv(T.AB, T.Z, T.H16, 128, 128 + BV, zk + ["H16"], ["ABb0"])
+            batch("v", [hl(T.Hs16[:, (r ^ 4):128:8], 32 * r, 32 * r + 16) for r in range(8)], [hk], "Hs16")
+            ga(T.AB, T.Z, T.H16, 128 + BV, 192, zk + ["H16"], ["ABb1"])
+            ga(T.AB, T.Z, T.H16, 192, 256, zk + ["H16"], ["ABb2"])
+            ga(T.AB, T.Z, T.H16, 0, 128, zk + ["H16"], ["ABa0", "ABa1"])
+            dma(T.Eb[:], T.AB[0:128:16, 2048:4096], ABK[2:], ["Eb"])
+            dma(T.Ea[:], T.AB[0:128:16, 0:2048], ABK[:2], ["Ea"])
+            pe_b = side_codes("Eb", "rb", "Pb")
+            if t < RO - 1:
+                op("a", act(T.rE[:], T["Iex%d" % t][:]), ["Iex"], ["rE"])
+            if t < 3:
+                lin([(T.Ps[:, 0:256], [(T.Ip, T.cod[:]), (T.Ip, T[X0][:])])], ["cod", X0], "Ps")
+            P0 = 0
+            for qi, np_ in enumerate(PQ):
+                lo, hi = 128 * P0, 128 * (P0 + np_)
+                bk = sorted(set(["ABb0" if 8 * P < BV else "ABb%d" % (1 + P // 8) for P in range(P0, P0 + np_)]))
+                if qi == len(PQ) - 2:
+                    pe_b()
+                    place_row(t)
+                    if t == 1:
+                        window(2, 0, 4)
+                    pe_a = side_codes("Ea", "ra", "Pa")
+                    if t == 1:
+                        window(2, 4, 8)
+                for M, L, W, mk in ((T.M1, T.H16, T.Wp, "M1"), (T.M2, T.Hs16, T.Wn, "M2")):
+                    key = "%s.%d" % (mk, qi)
+                    op("v", tt(M[:, lo:hi], T.Z[:].indirect(L[:, lo // 16:hi // 16]), T.AB[:, 2048 + lo:2048 + hi], A.max),
+                       zk + ["H16", "Hs16"] + bk, [key])
+                    sums([(P, W, M[:, 128 * P + 64 * j:128 * P + 64 * j + 64]) for P in range(P0, P0 + np_) for j in (0, 1)],
+                         [key], mk == "M2" and qi == len(PQ) - 1)
+                P0 += np_
+            pe_a()
+            dma(T.ZD[0:128:16, :], T["Iin%d" % t][:], ["Iin%d" % t], ["ZD0", "ZDv", "ZDa"])
+            if t < RO - 1:
+                lin([(T.Pe[:, 0:256], [(T.Ip, T["Iex%d" % t][:]), (T.Jn, T.rE[:]), (T.Ip, T[X1][:])])],
+                    ["Iex", "rE", X1], "Pe")
+                inverse_row(t)
+            if t == 1:
+                window(2, 8, 16)
+            val = lambda sd, j: (T.Pb if sd else T.Pa)[:, 64 * j:64 * j + 64]
+            da, db, ka, kb = T.Pa[:, 128:192], T.Pb[:, 128:192], ["Pa"], ["Pb"]
+        else:
+            op("v", cp(T.bb[:, 0:1024], T.xs[:].indirect(T.H16[:, 128:192])), ["xs", "H16"], ["bb0"])
+            op("a", act(T.bb[:, 1024:2048], T.xs[:].indirect(T.H16[:, 192:256])), ["xs", "H16"], ["bb1"])
+            op("v", tt(T.db[:], role(0, 1, 1), role(0, 1, 0), A.subtract), ["N"], ["db"])
+            op("v", tt(T.da[:], role(0, 0, 1), role(0, 0, 0), A.subtract), ["N"], ["da"])
+            for j in (0, 1):
+                for M, L, W, mk in ((T.M1, T.H16, T.Wp, "M1"), (T.M2, T.Hs16, T.Wn, "M2")):
+                    key = "%s.j%d" % (mk, j)
+                    op("v", tt(M[:, 1024 * j:1024 * j + 1024], T.xs[:].indirect(L[:, 64 * j:64 * j + 64]),
+                               T.bb[:, 1024 * j:1024 * j + 1024], A.max), ["xs", "H16", "Hs16", "bb%d" % j], [key])
+                    sums([(P, W, M[:, 1024 * j + P:1024 * j + 1024:16]) for P in range(16)], [key], mk == "M2" and j == 1)
+            op("v", ts(T.cod[:], T.c16[:], T.pc[:], 1.0 / 4096.0, A.add, A.mult), ["c16", "pc"], ["cod"])
+            batch("v", [ts(W[:], T.dg[:], 0.0, sg, A.is_equal, A.mult)
+                        for W, sg in ((T.Ip, 1.0), (T.In, -1.0), (T.Jp, 1.0), (T.Jn, -1.0))], ["dg"], "ident")
+            for mk in ("M1", "M2"):
+                for qi in range(len(PQ)):
+                    rd["%s.%d" % (mk, qi)] = {"cp": top["cp"]}
+            val = lambda sd, j: role(0, sd, j)
+            da, db, ka, kb = T.da[:], T.db[:], ["N", "da"], ["N", "db"]
+        op("v", ts(T.s[:], T.D[:, 0:64], 0.0, None, A.is_gt), ["D"], ["s"])
+        op("v", tt(T.eb[:], db, T.s[:], A.mult), kb + ["s"], ["eb"])
+        batch("v", [tt(brole(t, 0, 0), val(1, 0), T.eb[:], A.add), tt(brole(t, 0, 1), val(1, 1), T.eb[:], A.subtract)],
+              kb + ["eb"], "Bb")
+        op("v", tt(T.ea[:], da, T.s[:], A.mult), ka + ["s"], ["ea"])
+        batch("v", [tt(brole(t, 1, 0), val(0, 1), T.ea[:], A.subtract), tt(brole(t, 1, 1), val(0, 0), T.ea[:], A.add)],
+              ka + ["ea"], "Ba")
+        Bt, Bo = T["B%d" % t][:], T["Bout%d" % t][:]
+        op("v", code(Bo, Bt) if t else cp(Bo, Bt), ["Ba", "Bb"], ["Bout"])
+        send([T["Bout%d" % t]], T["Bin%d" % t], ["b%d_0" % t, "b%d_1" % t], ["Bout"])
+        N = T["N%d" % t]
+        if t:
+            batch("v", [code(role(t, sd, j), val(sd, j)) for sd in (0, 1) for j in (0, 1)], ["Pa", "Pb"], "N")
+        if t == RO - 1:
+            op("v", cp(T.o16[:], N[:]), ["N"], ["o16"])
+        else:
+            calls = []
+            for r in range(8):
+                c7, r4, tb = r >> 2, (r >> 1) & 1, r & 1
+                if t <= 3:
+                    sp = 2 ** (4 - t)
+                    h0 = (2 * c7 + r4) * sp
+                    src = N[:, h0 + tb:h0 + sp:2, :, :] if t < 3 else N[:, h0 + tb, :, :]
+                else:
+                    src = N[:, 2 * c7 + tb, r4, :]
+                calls.append(cp(T.o16[:, r:256:8], src))
+            batch("v", calls, ["N"], "o16")
+        iin = "Iin%d" % t
+        if t == 0:
+            dma(T.ZD[0:128:16, :], T[iin][:], [iin], ["ZD0", "ZDv", "ZDa"])
+            op("a", act(T.X00[:], T.xb0[:], OFF), ["xb0"], ["X00"])
+            op("a", act(T.X01[:], T.xb1[:], OFF), ["xb1"], ["X01"])
+            window(0)
+            window(1)
+            lin([(T.Ps[:, 0:256], [(T.Ip, T.cod[:]), (T.Ip, T.X00[:])]),
+                 (T.Ph[:, 0:256], [(T.Ip, T.Tv[:]), (T.Ip, T.Ta[:])])], ["cod", X0, "Tv", "Ta"], "Ps")
+            wr["Ph"] = dict(wr["Ps"])
+            op("v", ts(T.ti[:], T.Ph[:, 0:256], 0.25 - LIFT, None, A.add), ["Ph"], ["ti"])
+            op("v", ts(T.et[:], T.ti[:], -MID, 1.0 / 4096.0, A.add, A.mult), ["ti"], ["et"])
+            lin([(T.Pe[:, 0:256], [(T.Ip, T.et[:]), (T.Ip, T.X01[:])])], ["et", X1], "Pe")
+            place_row(0)
+            inverse_row(0)
+        elif t < RO - 1:
+            op("a", act(T.rL[:], T[iin][:], 0.5), [iin], ["rL"])
+            lin([(T.Pl[:, 0:256], [(T.Ip, T[iin][:]), (T.Jn, T.rL[:])])], [iin, "rL"], "Pl")
+        gv(T.AB, T.ZD, T.o16, 0, HV, ["ZD0", "o16"], ["ABa0"])
+        ga(T.AB, T.ZD, T.o16, HV, 256, ["ZD0", "o16"], ABK[1:])
+        dma(T.Hf[:], T.AB[0:128:16, :], ABK, ["Hf"])
+        if t == 0:
+            op("v", ts(T.tk[:], T.Iin0[:], 2048.25 - LIFT, None, A.add), [iin], ["tk"])
+            op("v", ts(T.tl[:], T.tk[:], 4095, None, A.bitwise_and), ["tk"], ["tl"])
+            op("v", cp(T.L16[:], T.tl[:]), ["tl"], ["L16"])
+        elif t < RO - 1:
+            op("v", code(T.L16[:], T.Pl[:, 0:256], 2048.0), ["Pl"], ["L16"])
+        if t < 2:
+            rows(t + 1)
+    need("g", top)

@@ -3,13 +3,14 @@ from concourse.mybir import AluOpType, ActivationFunctionType
 
 HOPS = (1, 3, 1, 3, 1, 3)
 RO = len(HOPS)
-NV = 96
-HV = 120
+NB = 5
+NG = 5
+B0 = 128
+HV = 124
 GV = 128
-IV = 132
-BV = 32
-PQ = (4, 4, 4, 2, 2)
-NDMA = 60
+IV = 128
+W2 = 10
+NDMA = 76
 
 F, I, U, B = "float32", "int32", "uint16", "bfloat16"
 SCRATCH = {
@@ -17,32 +18,29 @@ SCRATCH = {
     "V2": ("sbuf", [128, 4096], F), "Z": ("sbuf", [128, 4096], F), "GO": ("sbuf", [128, 4096], F),
     "AB": ("sbuf", [128, 4096], F), "ZD": ("sbuf", [128, 4096], F), "CW": ("sbuf", [128, 4096], F),
     "M1": ("sbuf", [128, 2048], B), "M2": ("sbuf", [128, 2048], B), "bb": ("sbuf", [128, 2048], B),
-    "G": ("sbuf", [128, 256], I), "G16": ("sbuf", [128, 256], U), "Gr": ("sbuf", [128, 256], F),
-    "Y": ("sbuf", [128, 16, 32], F), "Yt": ("sbuf", [128, 16, 32], F), "zero": ("sbuf", [128, 256], F),
+    "G": ("sbuf", [128, 256], I), "Gt": ("sbuf", [128, 8, 32], F),
     "pi": ("sbuf", [128, 1], I), "pj": ("sbuf", [128, 1], I), "pk": ("sbuf", [128, 1], I),
     "m0": ("sbuf", [128, 1], F), "m1": ("sbuf", [128, 1], F), "pc": ("sbuf", [128, 1], F),
     "Wp": ("sbuf", [128, 144], B), "Wn": ("sbuf", [128, 144], B),
-    "dg": ("sbuf", [128, 128], F), "Ip": ("sbuf", [128, 128], F), "In": ("sbuf", [128, 128], F),
-    "Jp": ("sbuf", [128, 128], B), "Jn": ("sbuf", [128, 128], B),
-    "c16": ("sbuf", [128, 256], F), "cod": ("sbuf", [128, 256], F),
-    "xb0": ("sbuf", [128, 256], B), "xb1": ("sbuf", [128, 256], B),
-    "st": ("sbuf", [128, 256], F), "emb": ("sbuf", [128, 256], F), "et": ("sbuf", [128, 256], F),
-    "ti": ("sbuf", [128, 256], I), "tk": ("sbuf", [128, 256], I), "tl": ("sbuf", [128, 256], I),
-    "rE": ("sbuf", [128, 256], B), "rL": ("sbuf", [128, 256], B), "rH": ("sbuf", [128, 256], B),
+    "dg": ("sbuf", [128, 128], F), "Ip": ("sbuf", [128, 128], F), "Jn": ("sbuf", [128, 128], B),
+    "Sel": ("sbuf", [128, 4, 128], F),
+    "rH": ("sbuf", [128, 2, 4, 32], B), "Hf": ("sbuf", [128, 2, 4, 32], F), "Hg": ("sbuf", [128, 2, 4, 32], F),
     "ra": ("sbuf", [128, 128], B), "rb": ("sbuf", [128, 128], B),
-    "H16": ("sbuf", [128, 256], U), "Hs16": ("sbuf", [128, 128], U), "o16": ("sbuf", [128, 256], U),
-    "L16": ("sbuf", [128, 256], U), "Hf": ("sbuf", [128, 256], F),
     "Ea": ("sbuf", [128, 128], F), "Eb": ("sbuf", [128, 128], F),
-    "da": ("sbuf", [128, 64], F), "db": ("sbuf", [128, 64], F), "ea": ("sbuf", [128, 64], F),
-    "eb": ("sbuf", [128, 64], F), "s": ("sbuf", [128, 64], F),
-    "Tv": ("sbuf", [128, 256], F), "Ta": ("sbuf", [128, 256], F),
-    "D": ("psum", [128, 512], F), "Pa": ("psum", [128, 512], F), "Pb": ("psum", [128, 512], F),
-    "Pe": ("psum", [128, 512], F), "Ps": ("psum", [128, 512], F), "Pl": ("psum", [128, 512], F),
-    "Ph": ("psum", [128, 512], F),
 }
-for _w in range(3):
-    SCRATCH["X%d0" % _w] = ("sbuf", [128, 256], F)
-    SCRATCH["X%d1" % _w] = ("sbuf", [128, 256], F)
+for _n in ("a0", "b0", "da", "db", "ea", "eb"):
+    SCRATCH[_n] = ("sbuf", [128, 64], F)
+for _n in ("Gr", "zero", "c16", "cod", "st", "emb", "et", "Tv", "Ta", "Jin", "Kin",
+           "X00", "X01", "X10", "X11", "X12", "X20", "X21"):
+    SCRATCH[_n] = ("sbuf", [128, 256], F)
+for _n in ("rE", "rL"):
+    SCRATCH[_n] = ("sbuf", [128, 256], B)
+for _n in ("ti", "tk"):
+    SCRATCH[_n] = ("sbuf", [128, 256], I)
+for _n in ("G16", "H16", "o16", "L16"):
+    SCRATCH[_n] = ("sbuf", [128, 256], U)
+for _n in ("D", "Pa", "Pb", "Pc", "Pe", "Pk", "Pl", "Ph"):
+    SCRATCH[_n] = ("psum", [128, 512], F)
 for _t in range(RO):
     SCRATCH["N%d" % _t] = ("sbuf", [128, 2 ** (6 - _t), 2, 2 ** (_t + 1)], U if _t else F)
     SCRATCH["B%d" % _t] = ("sbuf", [128, 2 ** (7 - _t), 2, 2 ** _t] if _t else [128, 128, 2], F)
@@ -52,7 +50,7 @@ for _t in range(RO):
     if _t:
         SCRATCH["Iex%d" % _t] = ("sbuf", [128, 256], F)
 
-SEMAPHORES = (["cv", "ca", "cp", "cg", "sent"] + ["d%d" % _i for _i in range(NDMA)]
+SEMAPHORES = (["cv", "ca", "cp", "cg", "sent", "j0", "kin"] + ["d%d" % _i for _i in range(NDMA)]
               + ["b%d_%d" % (_t, _h) for _t in range(RO) for _h in range(2)] + ["i%d" % _t for _t in range(RO)])
 
 OFF = 192.0
@@ -85,7 +83,8 @@ def helper_program(g, core, owner, half, T, topo):
     for t in range(RO):
         dst = T.cores[(r + HOPS[t]) % n]
         rid, pid = topo.addr(dst, core)
-        for buf, sem in (("Iin%d" % t, "i%d" % t), ("Bin%d" % t, "b%d_%d" % (t, half))):
+        tiles = [("Iin%d" % t, "i%d" % t), ("Bin%d" % t, "b%d_%d" % (t, half))]
+        for buf, sem in ([] if t else [("Jin", "j0")]) + tiles:
             g.wait_ge(T.sem[sem], got)
             g.remote_dma(T[buf][:, cols], T[buf][:, cols], T.sem[sem], T.sem.sent, pid, rid, topo.mask(core, dst))
             total += len(topo.engines(core, dst))
@@ -106,7 +105,7 @@ def rank_program(g, core, T, topo):
     ACT = ActivationFunctionType
     Q = {"v": g.vector, "a": g.scalar, "p": g.tensor, "g": g, "s": g.sync}
     seen = {q: {} for q in Q}
-    wr, rd, top = {}, {}, {}
+    wr, rd, top = {}, {}, {"sent": 0}
     ndma = [0]
 
     def need(q, toks):
@@ -151,7 +150,7 @@ def rank_program(g, core, T, topo):
 
     hs = helpers(core, T, topo)
 
-    def send(srcs, land, sems, reads):
+    def send(src, land, sems, reads):
         order("g", reads, [])
         tr = []
         for h in range(2):
@@ -159,24 +158,24 @@ def rank_program(g, core, T, topo):
             e = e[h * len(e) // 2:(h + 1) * len(e) // 2]
             rid, pid = topo.addr(hs[h], core)
             cols = slice(128 * h, 128 * h + 128)
-            to = [DstId(rid=rid, pnc=pid)]
-            if len(srcs) == 1:
-                tr.append(RemoteDMATransfer(dst_ids=to, dma_engine_mask=bits(e), remote_sem=T.sem[sems[h]],
-                                            src=srcs[0][:, cols], dst=land[:, cols]))
-            else:
-                tr.append(RemoteDMATransfer(dst_ids=to, dma_engine_mask=bits(e), remote_sem=T.sem[sems[h]],
-                                            srcs=[x[:, cols] for x in srcs], dsts=[land[:, cols]], alu_op=1))
-            top["sent"] = top.get("sent", 0) + len(e)
+            tr.append(RemoteDMATransfer(dst_ids=[DstId(rid=rid, pnc=pid)], dma_engine_mask=bits(e),
+                                        remote_sem=T.sem[sems[h]], src=src[:, cols], dst=land[:, cols]))
+            top["sent"] += len(e)
         g.remote_dma_fused(tr, local_sem=T.sem.sent)
 
+    def lands(key, sem, count):
+        wr[key] = {sem: count}
+        top[sem] = count
+
+    far = HOPS[-2] + HOPS[-1]
+    lands("Kin", "kin", len(topo.engines(T.cores[(rank - far) % n], core)))
     for t in range(RO):
-        src = T.cores[(rank - HOPS[t]) % n]
-        cnt = [len(topo.engines(h, core)) for h in helpers(src, T, topo)]
-        wr["Iin%d" % t] = {"i%d" % t: sum(cnt)}
-        top["i%d" % t] = sum(cnt)
+        cnt = [len(topo.engines(h, core)) for h in helpers(T.cores[(rank - HOPS[t]) % n], T, topo)]
+        lands("Iin%d" % t, "i%d" % t, sum(cnt))
+        if t == 0:
+            lands("Jin", "j0", sum(cnt))
         for h in range(2):
-            wr["Bin%d_%d" % (t, h)] = {"b%d_%d" % (t, h): cnt[h]}
-            top["b%d_%d" % (t, h)] = cnt[h]
+            lands("Bin%d_%d" % (t, h), "b%d_%d" % (t, h), cnt[h])
 
     V, S = g.vector, g.scalar
 
@@ -191,10 +190,10 @@ def rank_program(g, core, T, topo):
     def tt(out, a, b, o):
         return lambda: V.tensor_tensor(out, a, b, o)
 
-    def act(out, in_, bias=None):
+    def act(out, in_, bias=None, func=None):
         if bias is None:
-            return lambda: S.activation(out, in_, ACT.Identity)
-        return lambda: S.activation(out, in_, ACT.Identity, bias=float(bias))
+            return lambda: S.activation(out, in_, func or ACT.Identity)
+        return lambda: S.activation(out, in_, func or ACT.Identity, bias=float(bias))
 
     def code(out, frac, extra=0.0):
         return ts(out, frac, 4096.0, MID + extra, A.mult, A.add)
@@ -202,15 +201,17 @@ def rank_program(g, core, T, topo):
     def gv(out, win, lst, a, b, reads, keys):
         op("v", cp(out[:, 16 * a:16 * b], win[:].indirect(lst[:, a:b])), reads, keys)
 
-    def ga(out, win, lst, a, b, reads, keys, also=()):
-        op("a", act(out[:, 16 * a:16 * b], win[:].indirect(lst[:, a:b])), reads, keys, also)
+    def ga(out, win, lst, a, b, reads, keys):
+        op("a", act(out[:, 16 * a:16 * b], win[:].indirect(lst[:, a:b])), reads, keys)
 
     def lin(groups, reads, key):
         calls = []
         for out, terms in groups:
             for i, (W, x) in enumerate(terms):
-                calls.append(lambda out=out, W=W, x=x, a=(i == 0), z=(i == len(terms) - 1): g.tensor.matmul(out, W[:], x, a, z))
+                calls.append(lambda out=out, W=W, x=x, a=(i == 0), z=(i == len(terms) - 1): g.tensor.matmul(out, W, x, a, z))
         batch("p", calls, reads + ["ident"], key)
+
+    Ip, Jn = T.Ip[:], T.Jn[:]
 
     def role(t, side, j):
         return T["N%d" % t][:, :, side, j::2] if t else T.N0[:, :, side, j]
@@ -218,6 +219,9 @@ def rank_program(g, core, T, topo):
     def brole(t, side, j):
         hi = 2 ** (6 - t)
         return T["B%d" % t][:, j * hi:(j + 1) * hi, side, :] if t else T.B0[:, j * hi:(j + 1) * hi, side]
+
+    def blk(side, j):
+        return 64 * (2 * j + side)
 
     first_mm = [True]
 
@@ -228,27 +232,46 @@ def rank_program(g, core, T, topo):
             op("p", lambda: g.tensor.matmul(T.D[:, 0:64], W[:, 16 - P:144 - P], rhs, st, fin),
                reads + ["Wp", "Wn"], ["D"] if st else [], [] if st else ["D"])
 
-    ABK = ["ABa0", "ABa1", "ABb0", "ABb1", "ABb2"]
+    done = [0, 0, 0]
 
+    def window(w, upto):
+        Vw = T["V%d" % w]
+        for u in range(done[w], upto):
+            run, step = slice(256 * u, 256 * u + 256), slice(u, 4096, 16)
+            out, in_ = ((run, run), (step, run), (run, step))[w]
+            op("a", act(Vw[:, out], T.xs[:, in_], OFF), ["xs"], [] if u else ["V%d" % w], ["V%d" % w] if u else [])
+        done[w] = upto
+
+    def rows(w, ps):
+        for p in ps:
+            dma(T["X%d%d" % (w, p)][:], T["V%d" % w][p:128:16, :], ["V%d" % w], ["X%d%d" % (w, p)])
+
+    def ride(w, p, tile):
+        Vn = "V%d" % w
+        dma(T[Vn][p:128:16, :], T[tile][:], [tile, Vn, "X%d%d" % (w, p)], ["%s.%d" % (Vn, p)])
+
+    def place_row(w):
+        op("v", tt(T.st[:], T.cod[:], T["X%d0" % w][:], A.add), ["cod", "X%d0" % w], ["st"])
+        ride(w, 0, "st")
+
+    NV = 16 * NB
+    small = dict(allow_small_or_imprecise_dtypes=True)
     dma(T.G[:], T.o[:], [], ["G"])
-    op("g", lambda: g.iota(T.ZD[:, 0:256], [[16, 128], [2048, 2]], int(LIFT), 0, allow_small_or_imprecise_dtypes=True),
-       [], ["ZD0"])
+    op("g", lambda: g.iota(T.ZD[:, 0:256], [[16, 128], [2048, 2]], int(LIFT), 0, **small), [], ["ZD0"])
     op("g", lambda: g.iota(T.pi[:], [[1, 1]], 0, 1), [], ["pi"])
-    op("g", lambda: g.iota(T.c16[:], [[16, 256]], 0, 0, allow_small_or_imprecise_dtypes=True), [], ["c16"])
-    op("g", lambda: g.iota(T.dg[:], [[1, 128]], 0, -1, allow_small_or_imprecise_dtypes=True), [], ["dg"])
-    op("g", lambda: g.iota(T.CW[:], [[1, 16], [16, 256]], 0, 0, allow_small_or_imprecise_dtypes=True), [], ["CW"])
+    op("g", lambda: g.iota(T.dg[:], [[1, 128]], 0, -1, **small), [], ["dg"])
+    op("g", lambda: g.iota(T.ZD[:, 256 * NB:256 * (NB + NG)], [[1, NG], [16, 128], [2048, 2]], int(LIFT) + NB, 0, **small),
+       [], ["ZDg"])
+    op("g", lambda: g.iota(T.c16[:], [[16, 256]], 0, 0, **small), [], ["c16"])
+    op("g", lambda: g.iota(T.ZD[:, 256:256 * NB], [[0, 256 * (NB - 1)]], 0, 0, **small), [], ["ZDf"])
     op("v", lambda: V.memset(T.zero[:], 0.0), [], ["zero"])
     dma(T.Z[0:128:16, :], T.zero[:], ["zero"], ["Z.v"])
     dma(T.GO[0:128:16, :], T.zero[:], ["zero"], ["GO.a"])
     dma(T.xs[:], T.x[:], [], ["xs"])
-    dma(T.xb0[:], T.x[0:128:16, :], [], ["xb0"])
-    dma(T.xb1[:], T.x[1:128:16, :], [], ["xb1"])
+    batch("a", [act(T.ZD[:, 256 * P:256 * P + 256], T.ZD[:, 0:256], P, ACT.Silu) for P in range(NB + NG, 16)],
+          ["ZD0"], "ZDa")
     op("v", lambda: V.memset(T.Wp[:], 0.0), [], ["Wp"])
     op("v", lambda: V.memset(T.Wn[:], 0.0), [], ["Wn"])
-    nb = NV // 16
-    batch("v", [ts(T.ZD[:, 256 * P:256 * P + 256], T.ZD[:, 0:256], float(P), None, A.add) for P in range(1, nb)],
-          ["ZD0"], "ZDv")
-    batch("a", [act(T.ZD[:, 256 * P:256 * P + 256], T.ZD[:, 0:256], P) for P in range(nb, 16)], ["ZD0"], "ZDa")
     op("v", lambda: V.memset(T.Wp[:, 0:144:16], 1.0), [], ["Wp"])
     op("v", lambda: V.memset(T.Wn[:, 0:144:16], -1.0), [], ["Wn"])
     op("v", ts(T.pj[:], T.pi[:], 4, 1, A.logical_shift_right, A.bitwise_and), ["pi"], ["pj"])
@@ -256,168 +279,185 @@ def rank_program(g, core, T, topo):
     op("v", cp(T.m1[:], T.pj[:]), ["pj"], ["m1"])
     op("v", ts(T.m0[:], T.pj[:], -1.0, 1.0, A.mult, A.add), ["pj"], ["m0"])
     op("v", ts(T.pc[:], T.pk[:], -MID, None, A.add), ["pk"], ["pc"])
+    batch("v", [ts(T.Sel[:, 2 * q + c, :], T.dg[:], 16.0 * (c - q), (T.m0, T.m1)[q][:], A.is_equal, A.mult)
+                for q in (0, 1) for c in (0, 1)], ["dg", "m0", "m1"], "ident")
     op("v", cp(T.G16[:], T.G[:]), ["G"], ["G16"])
     op("a", lambda: S.activation(T.GO[:].indirect(T.G16[:, NV:256]), T.ZD[:, 16 * NV:4096], ACT.Silu),
-       ["G16", "ZDa"], ["GO.a"])
-    op("v", cp(T.Z[:].indirect(T.G16[:, 0:NV]), T.ZD[:, 0:16 * NV]), ["G16", "ZD0", "ZDv"], ["Z.v"])
+       ["G16", "ZDa", "ZDg"], ["GO.a"])
+    batch("v", [cp(T.Gr[:, 32 * (u & 7) + 16 * (u >> 3):32 * (u & 7) + 16 * (u >> 3) + 16], T.G[:, u:256:16])
+                for u in range(16)], ["G"], "Gr")
+    batch("v", [(lambda u=u: V.transpose(T.Gt[:, u, :], T.Gr[:, 32 * u:32 * u + 32])) for u in range(8)], ["Gr"], "Gt")
+    lin([(T.Pa[:, 128 * q:128 * q + 128], [(T.Sel[:, 2 * q + c, :], T.Gt[:, :, 16 * c:16 * c + 16]) for c in (0, 1)])
+         for q in (0, 1)], ["Gt"], "Pa")
+    for P in range(NB):
+        op("v", ts(T.Z[:].indirect(T.G16[:, 16 * P:16 * P + 16]), T.ZD[:, 0:256], 1.0, float(P), A.mult, A.add),
+           ["G16", "ZD0"], ["Z.v"])
     dma(T.Tv[:], T.Z[0:128:16, :], ["Z.v"], ["Tv"])
+    send(T.Tv, T.Jin, ["j0", "j0"], ["Tv"])
     dma(T.Ta[:], T.GO[0:128:16, :], ["GO.a"], ["Ta"])
+    send(T.Ta, T.Iin0, ["i0", "i0"], ["Ta"])
     rd["Z.a"], rd["GO.v"] = dict(rd["Z.v"]), dict(rd["GO.a"])
-    send([T.Tv, T.Ta], T.Iin0, ["i0", "i0"], ["Tv", "Ta"])
-    batch("v", [cp(T.Gr[:, 16 * u:16 * u + 16], T.G[:, u:256:16]) for u in range(16)], ["G"], "Gr")
-    batch("v", [ts(T.Y[:, :, 0:16], T.Gr[:], T.m0[:], None, A.mult),
-                ts(T.Y[:, :, 16:32], T.Gr[:], T.m1[:], None, A.mult)], ["Gr", "m0", "m1"], "Y")
-    batch("v", [(lambda u=u: V.transpose(T.Yt[:, u, :], T.Y[:, u, :])) for u in range(16)], ["Y"], "Yt")
-    op("v", tt(T.N0[:], T.Yt[:, :, 0:16], T.Yt[:, :, 16:32], A.add), ["Yt"], ["N"])
-    batch("v", [cp(T.H16[:, 128 * sd + 64 * j:128 * sd + 64 * j + 64], role(0, sd, j)) for sd in (1, 0) for j in (0, 1)],
-          ["N"], "H16")
-    batch("v", [cp(T.Hs16[:, 64 * (1 - j):64 * (1 - j) + 64], role(0, 0, j)) for j in (0, 1)], ["N"], "Hs16")
-
-    def window(w, a=0, b=16):
-        Vw = T["V%d" % w]
-        if w == 0:
-            pairs = [(Vw[:], T.xs[:])]
-        elif w == 1:
-            pairs = [(Vw[:, u:4096:16], T.xs[:, 256 * u:256 * u + 256]) for u in range(16)]
-        else:
-            pairs = [(Vw[:, 256 * u:256 * u + 256], T.xs[:, u:4096:16]) for u in range(16)]
-        for k in range(a, min(b, len(pairs))):
-            op("a", act(pairs[k][0], pairs[k][1], OFF), ["xs"], [] if k else ["V%d" % w], ["V%d" % w] if k else [])
-
-    def rows(w):
-        for p in range(2):
-            dma(T["X%d%d" % (w, p)][:], T["V%d" % w][p:128:16, :], ["V%d" % w], ["X%d%d" % (w, p)])
-
-    def side_codes(E, r, P):
-        op("a", act(T[r][:], T[E][:]), [E], [r])
-        return lambda: lin([(T[P][:, 0:128], [(T.Ip, T[E][:]), (T.Jn, T[r][:])]),
-                            (T[P][:, 128:192], [(T.Ip, T[E][:, 64:128]), (T.In, T[E][:, 0:64]),
-                                                (T.Jn, T[r][:, 64:128]), (T.Jp, T[r][:, 0:64])])], [E, r], P)
-
-    def inverse_row(t):
-        Vn = "V%d" % (t % 3)
-        op("a", act(T.emb[:], T.Pe[:, 0:256]), ["Pe"], ["emb"])
-        dma(T[Vn][1:128:16, :], T.emb[:], ["emb", Vn], [Vn + "i"])
-
-    def place_row(t):
-        Vn = "V%d" % (t % 3)
-        if t < 3:
-            op("a", act(T.st[:], T.Ps[:, 0:256]), ["Ps"], ["st"])
-            dma(T[Vn][0:128:16, :], T.st[:], ["st", Vn], [Vn + "c"])
+    batch("v", [cp(T.H16[:, blk(sd, j):blk(sd, j) + 64], T.Pa[:, 2 * sd + j:256:4]) for sd in (1, 0) for j in (0, 1)],
+          ["Pa"], "H16")
 
     zk = ["Z.v", "Z.a"]
+    gk = ["GO.v", "GO.a"]
+    j0, j1 = slice(0, 64), slice(64, 128)
     for t in range(RO + 1):
-        w = (t - 1) % 3
-        X0, X1 = "X%d0" % (t % 3), "X%d1" % (t % 3)
+        w, iex, iin = t % 3, "Iex%d" % t, "Iin%d" % t
         if t > 0:
-            win, wk = (T["V%d" % w], ["V%d" % w, "V%dc" % w, "V%di" % w]) if t < RO else (T.CW, ["CW"])
+            Vn = "V%d" % ((t - 1) % 3) if t < RO else "CW"
+            wk = [Vn] + ["%s.%d" % (Vn, p) for p in range(3)]
             b0, b1 = "Bin%d_0" % (t - 1), "Bin%d_1" % (t - 1)
             Bin = T["Bin%d" % (t - 1)]
-            gv(T.Z, win, Bin, 0, GV, wk + [b0] + ([b1] if GV > 128 else []), ["Z.v"])
-            ga(T.Z, win, Bin, GV, 256, wk + [b1] + ([b0] if GV < 128 else []), ["Z.a"])
-
-            def round_h():
+            gv(T.Z, T[Vn], Bin, 0, GV, wk + [b0] + ([b1] if GV > 128 else []), ["Z.v"])
+            ga(T.Z, T[Vn], Bin, GV, 256, wk + [b1] + ([b0] if GV < 128 else []), ["Z.a"])
+            if t > 1:
                 op("a", act(T.rH[:], T.Hf[:]), ["Hf"], ["rH"])
-                lin([(T.Ph[:, 0:256], [(T.Ip, T.Hf[:]), (T.Jn, T.rH[:])])], ["Hf", "rH"], "Ph")
-
             if t == RO:
-                round_h()
+                lin([(T.Ph[:, 0:256], [(Ip, T.Hf[:]), (Jn, T.rH[:])])], ["Hf", "rH"], "Ph")
                 op("v", code(T.H16[:], T.Ph[:, 0:256]), ["Ph"], ["H16"])
                 gv(T.GO, T.Z, T.H16, 0, 128, zk + ["H16"], ["GO.v"])
                 ga(T.GO, T.Z, T.H16, 128, 256, zk + ["H16"], ["GO.a"])
-                dma(T.yo[:], T.GO[0:128:16, :], ["GO.v", "GO.a"], [])
+                dma(T.yo[:], T.GO[0:128:16, :], gk, [])
                 break
-            gv(T.GO, T.Z, T.L16, 0, IV, zk + ["L16"], ["GO.v"])
-            mid = (IV + 256) // 4 * 2
-            ga(T.GO, T.Z, T.L16, IV, mid, zk + ["L16"], ["GO.a"])
-            if t > 1:
-                round_h()
-            ga(T.GO, T.Z, T.L16, mid, 256, zk + ["L16"], [], ["GO.a"])
-            dma(T["Iex%d" % t][:], T.GO[1:128:16, :], ["GO.v", "GO.a"], ["Iex"])
-            send([T["Iex%d" % t]], T["Iin%d" % t], ["i%d" % t] * 2, ["Iex"])
-            if t > 1:
-                hk = "Ph"
-                hl = lambda o, a, b: code(o, T.Ph[:, a:b])
+            W, other = (Jn, "rH") if t > 1 else (Ip, "Hg")
+            lin([(T.Ph[:, 64 * z:64 * z + 64], [(Ip, T.Hf[:, :, z, :]), (W, T[other][:, :, z, :])]) for z in range(4)],
+                ["Hf", other], "Ph")
+            if t < RO - 1:
+                gv(T.GO, T.Z, T.L16, 0, IV, zk + ["L16"], ["GO.v"])
+                ga(T.GO, T.Z, T.L16, IV, 256, zk + ["L16"], ["GO.a"])
+                dma(T[iex][:], T.GO[1:128:16, :], gk, ["Iex"])
             else:
-                hk = "Hf"
-                hl = lambda o, a, b: ts(o, T.Hf[:, a:b], 0.25 - LIFT, None, A.add)
-            batch("v", [hl(T.H16[:, r:256:8], 32 * r, 32 * r + 32) for r in range(8)], [hk], "H16")
-            gv(T.AB, T.Z, T.H16, 128, 128 + BV, zk + ["H16"], ["ABb0"])
-            batch("v", [hl(T.Hs16[:, (r ^ 4):128:8], 32 * r, 32 * r + 16) for r in range(8)], [hk], "Hs16")
-            ga(T.AB, T.Z, T.H16, 128 + BV, 192, zk + ["H16"], ["ABb1"])
-            ga(T.AB, T.Z, T.H16, 192, 256, zk + ["H16"], ["ABb2"])
-            ga(T.AB, T.Z, T.H16, 0, 128, zk + ["H16"], ["ABa0", "ABa1"])
-            dma(T.Eb[:], T.AB[0:128:16, 2048:4096], ABK[2:], ["Eb"])
-            dma(T.Ea[:], T.AB[0:128:16, 0:2048], ABK[:2], ["Ea"])
-            pe_b = side_codes("Eb", "rb", "Pb")
+                dma(T[iex][:], T.Z[1:128:16, :], zk, ["Iex"])
+            send(T[iex], T[iin], ["i%d" % t] * 2, ["Iex"])
+            if t == RO - 2:
+                dst = T.cores[(rank + far) % n]
+                rid, pid = topo.addr(dst, core)
+                g.remote_dma(T.Kin[:], T[iex][:], T.sem.kin, T.sem.sent, pid, rid, topo.mask(core, dst))
+                top["sent"] += len(topo.engines(core, dst))
+            if t > 1:
+                calls = [code(T.H16[:, z:256:4], T.Ph[:, 64 * z:64 * z + 64]) for z in range(4)]
+            else:
+                calls = [ts(T.H16[:, z:256:4], T.Ph[:, 64 * z:64 * z + 64], 0.25 - LIFT, None, A.add) for z in range(4)]
+            batch("v", calls, ["Ph"], "H16")
+            hk = zk + ["H16"]
+
+            def piece(eng, side, j, h, key):
+                a = blk(side, j) + 32 * h
+                eng(T.AB, T.Z, T.H16, a, a + (32 if side else 64), hk, [key])
+
+            def fold(out, p, side, j, key):
+                c = 16 * blk(side, j)
+                dma(out, T.AB[p:128:16, c:c + 1024], ["b%d0" % j, "b%d1" % j] if side else ["a%dr" % j], [key])
+
+            def fused(M, j, jb, p0, p1, last=False):
+                key = "%s.%d.%d" % (M, j, p0)
+                lo, a, b = 1024 * j, blk(0, j), 16 * blk(1, jb)
+                op("v", tt(T[M][:, lo + 64 * p0:lo + 64 * p1], T.Z[:].indirect(T.H16[:, a + 4 * p0:a + 4 * p1]),
+                           T.AB[:, b + 64 * p0:b + 64 * p1], A.max), hk + ["b%d%d" % (jb, p0 // 8)], [key])
+                sums([(P, T.Wp if M == "M1" else T.Wn, T[M][:, lo + 64 * P:lo + 64 * P + 64]) for P in range(p0, p1)],
+                     [key], last)
+
+            def whole(r, E, j):
+                op("a", act(T[r][:, (j0, j1)[j]], T[E][:, (j0, j1)[j]]), ["%s%d" % (E, j)], ["%s%d" % (r, j)])
+
+            piece(gv, 1, 0, 0, "b00")
+            piece(ga, 1, 1, 0, "b10")
+            piece(ga, 1, 0, 1, "b01")
+            fold(T.Eb[:, j0], 0, 1, 0, "Eb0")
+            piece(ga, 1, 1, 1, "b11")
+            fold(T.Eb[:, j1], 0, 1, 1, "Eb1")
+            piece(ga, 0, 0, 0, "a0r")
+            fold(T.Ea[:, j0], 0, 0, 0, "Ea0")
+            piece(ga, 0, 1, 0, "a1r")
+            fold(T.Ea[:, j1], 0, 0, 1, "Ea1")
+            kk = []
+            if t == RO - 1:
+                for sd, j in ((1, 0), (1, 1), (0, 0), (0, 1)):
+                    kk.append("K%d%d" % (sd, j))
+                    fold(T.et[:, blk(sd, j):blk(sd, j) + 64], 2, sd, j, kk[-1])
+            whole("rb", "Eb", 1)
+            whole("rb", "Eb", 0)
+            whole("ra", "Ea", 0)
+            whole("ra", "Ea", 1)
+            fused("M1", 0, 0, 0, 8)
+            fused("M2", 1, 0, 0, 8)
+            fused("M1", 1, 1, 0, 8)
+            fused("M2", 0, 1, 0, 8)
+            fused("M1", 0, 0, 8, 16)
+            fused("M2", 1, 0, 8, 16)
+            fused("M1", 1, 1, 8, 16)
+            lin([(T.Pb[:, j0], [(Ip, T.Eb[:, j1]), (Jn, T.rb[:, j1])])], ["Eb1", "rb1"], "Pb")
+            fused("M2", 0, 1, 8, 13)
+            fused("M2", 0, 1, 13, 16, True)
+            lin([(T.Pa[:, j0], [(Ip, T.Ea[:, j1]), (Jn, T.ra[:, j1])])], ["Ea1", "ra1"], "Pa")
+            op("v", tt(T.b0[:], T.Eb[:, j0], T.rb[:, j0], A.subtract), ["Eb0", "rb0"], ["b0"])
+            op("v", tt(T.a0[:], T.Ea[:, j0], T.ra[:, j0], A.subtract), ["Ea0", "ra0"], ["a0"])
+            op("v", tt(T.db[:], T.Pb[:, j0], T.b0[:], A.subtract), ["Pb", "b0"], ["db"])
+            dma(T.ZD[0:128:16, :], T[iin][:], [iin], ["ZD0"])
             if t < RO - 1:
-                op("a", act(T.rE[:], T["Iex%d" % t][:]), ["Iex"], ["rE"])
-            if t < 3:
-                lin([(T.Ps[:, 0:256], [(T.Ip, T.cod[:]), (T.Ip, T[X0][:])])], ["cod", X0], "Ps")
-            P0 = 0
-            for qi, np_ in enumerate(PQ):
-                lo, hi = 128 * P0, 128 * (P0 + np_)
-                bk = sorted(set(["ABb0" if 8 * P < BV else "ABb%d" % (1 + P // 8) for P in range(P0, P0 + np_)]))
-                if qi == len(PQ) - 2:
-                    pe_b()
-                    place_row(t)
-                    if t == 1:
-                        window(2, 0, 4)
-                    pe_a = side_codes("Ea", "ra", "Pa")
-                    if t == 1:
-                        window(2, 4, 8)
-                for M, L, W, mk in ((T.M1, T.H16, T.Wp, "M1"), (T.M2, T.Hs16, T.Wn, "M2")):
-                    key = "%s.%d" % (mk, qi)
-                    op("v", tt(M[:, lo:hi], T.Z[:].indirect(L[:, lo // 16:hi // 16]), T.AB[:, 2048 + lo:2048 + hi], A.max),
-                       zk + ["H16", "Hs16"] + bk, [key])
-                    sums([(P, W, M[:, 128 * P + 64 * j:128 * P + 64 * j + 64]) for P in range(P0, P0 + np_) for j in (0, 1)],
-                         [key], mk == "M2" and qi == len(PQ) - 1)
-                P0 += np_
-            pe_a()
-            dma(T.ZD[0:128:16, :], T["Iin%d" % t][:], ["Iin%d" % t], ["ZD0", "ZDv", "ZDa"])
-            if t < RO - 1:
-                lin([(T.Pe[:, 0:256], [(T.Ip, T["Iex%d" % t][:]), (T.Jn, T.rE[:]), (T.Ip, T[X1][:])])],
-                    ["Iex", "rE", X1], "Pe")
-                inverse_row(t)
-            if t == 1:
-                window(2, 8, 16)
-            val = lambda sd, j: (T.Pb if sd else T.Pa)[:, 64 * j:64 * j + 64]
-            da, db, ka, kb = T.Pa[:, 128:192], T.Pb[:, 128:192], ["Pa"], ["Pb"]
+                op("a", act(T.rE[:], T[iex][:]), ["Iex"], ["rE"])
+                lin([(T.Pe[:, 0:256], [(Ip, T[iex][:]), (Jn, T.rE[:])])], ["Iex", "rE"], "Pe")
+            else:
+                op("a", act(T.rE[:], T.et[:]), kk, ["rE"])
+                lin([(T.Pe[:, 0:256], [(Ip, T.et[:]), (Jn, T.rE[:])])], kk + ["rE"], "Pe")
+            if t < RO - 2:
+                op("a", act(T.rL[:], T[iin][:], 0.5), [iin], ["rL"])
+                lin([(T.Pl[:, 0:256], [(Ip, T[iin][:]), (Jn, T.rL[:])])], [iin, "rL"], "Pl")
+                if t == 1:
+                    window(2, 16)
+            elif t == RO - 2:
+                op("a", act(T.rL[:], T.Kin[:], 0.5), ["Kin"], ["rL"])
+                lin([(T.Pk[:, 0:256], [(Ip, T.Kin[:]), (Jn, T.rL[:]), (Ip, T.X12[:])])], ["Kin", "rL", "X12"], "Pk")
+                op("a", act(T.st[:], T.Pk[:, 0:256], 0.5), ["Pk"], ["st"])
+                ride(w, 2, "st")
+            val = lambda sd, j: ((T.a0[:], T.Pa[:, j0]), (T.b0[:], T.Pb[:, j0]))[sd][j]
+            ka, kb = ["Pa", "a0"], ["Pb", "b0"]
         else:
-            op("v", cp(T.bb[:, 0:1024], T.xs[:].indirect(T.H16[:, 128:192])), ["xs", "H16"], ["bb0"])
-            op("a", act(T.bb[:, 1024:2048], T.xs[:].indirect(T.H16[:, 192:256])), ["xs", "H16"], ["bb1"])
+            for eng, a, b in (("v", 0, B0), ("a", B0, 128)):
+                for j in (0, 1):
+                    lo, hi = max(a, 64 * j), min(b, 64 * j + 64)
+                    if lo < hi:
+                        c = blk(1, j) - 64 * j
+                        src, out = T.xs[:].indirect(T.H16[:, c + lo:c + hi]), T.bb[:, 16 * lo:16 * hi]
+                        op(eng, cp(out, src) if eng == "v" else act(out, src), ["xs", "H16"], ["bb%s%d" % (eng, j)])
+            window(0, 16)
+            rows(0, (0, 1))
+            window(1, 16)
+            window(2, W2)
+            for M, j, jb in (("M1", 0, 0), ("M2", 1, 0), ("M1", 1, 1), ("M2", 0, 1)):
+                keys = ["%s.%d.%d" % (M, j, p0) for p0 in (0, 8, 13)]
+                op("v", tt(T[M][:, 1024 * j:1024 * j + 1024], T.xs[:].indirect(T.H16[:, blk(0, j):blk(0, j) + 64]),
+                           T.bb[:, 1024 * jb:1024 * jb + 1024], A.max), ["xs", "H16", "bbv%d" % jb, "bba%d" % jb], keys)
+                sums([(P, T.Wp if M == "M1" else T.Wn, T[M][:, 1024 * j + P:1024 * j + 1024:16]) for P in range(16)],
+                     keys, (M, j) == ("M2", 0))
+            op("v", cp(T.N0[:], T.Pa[:, 0:256]), ["Pa"], ["N"])
             op("v", tt(T.db[:], role(0, 1, 1), role(0, 1, 0), A.subtract), ["N"], ["db"])
             op("v", tt(T.da[:], role(0, 0, 1), role(0, 0, 0), A.subtract), ["N"], ["da"])
-            for j in (0, 1):
-                for M, L, W, mk in ((T.M1, T.H16, T.Wp, "M1"), (T.M2, T.Hs16, T.Wn, "M2")):
-                    key = "%s.j%d" % (mk, j)
-                    op("v", tt(M[:, 1024 * j:1024 * j + 1024], T.xs[:].indirect(L[:, 64 * j:64 * j + 64]),
-                               T.bb[:, 1024 * j:1024 * j + 1024], A.max), ["xs", "H16", "Hs16", "bb%d" % j], [key])
-                    sums([(P, W, M[:, 1024 * j + P:1024 * j + 1024:16]) for P in range(16)], [key], mk == "M2" and j == 1)
-            op("v", ts(T.cod[:], T.c16[:], T.pc[:], 1.0 / 4096.0, A.add, A.mult), ["c16", "pc"], ["cod"])
-            batch("v", [ts(W[:], T.dg[:], 0.0, sg, A.is_equal, A.mult)
-                        for W, sg in ((T.Ip, 1.0), (T.In, -1.0), (T.Jp, 1.0), (T.Jn, -1.0))], ["dg"], "ident")
-            for mk in ("M1", "M2"):
-                for qi in range(len(PQ)):
-                    rd["%s.%d" % (mk, qi)] = {"cp": top["cp"]}
             val = lambda sd, j: role(0, sd, j)
-            da, db, ka, kb = T.da[:], T.db[:], ["N", "da"], ["N", "db"]
-        op("v", ts(T.s[:], T.D[:, 0:64], 0.0, None, A.is_gt), ["D"], ["s"])
-        op("v", tt(T.eb[:], db, T.s[:], A.mult), kb + ["s"], ["eb"])
+            ka, kb = ["N"], ["N"]
+        s = T.Pc[:, j0]
+        op("v", ts(s, T.D[:, j0], 0.0, None, A.is_gt), ["D"], ["s"])
+        if t:
+            op("v", tt(T.da[:], val(0, 1), val(0, 0), A.subtract), ka, ["da"])
+        op("v", tt(T.eb[:], T.db[:], s, A.mult), ["db", "s"], ["eb"])
+        op("v", tt(T.ea[:], T.da[:], s, A.mult), ["da", "s"], ["ea"])
         batch("v", [tt(brole(t, 0, 0), val(1, 0), T.eb[:], A.add), tt(brole(t, 0, 1), val(1, 1), T.eb[:], A.subtract)],
               kb + ["eb"], "Bb")
-        op("v", tt(T.ea[:], da, T.s[:], A.mult), ka + ["s"], ["ea"])
         batch("v", [tt(brole(t, 1, 0), val(0, 1), T.ea[:], A.subtract), tt(brole(t, 1, 1), val(0, 0), T.ea[:], A.add)],
               ka + ["ea"], "Ba")
         Bt, Bo = T["B%d" % t][:], T["Bout%d" % t][:]
         op("v", code(Bo, Bt) if t else cp(Bo, Bt), ["Ba", "Bb"], ["Bout"])
-        send([T["Bout%d" % t]], T["Bin%d" % t], ["b%d_0" % t, "b%d_1" % t], ["Bout"])
+        send(T["Bout%d" % t], T["Bin%d" % t], ["b%d_0" % t, "b%d_1" % t], ["Bout"])
         N = T["N%d" % t]
-        if t:
-            batch("v", [code(role(t, sd, j), val(sd, j)) for sd in (0, 1) for j in (0, 1)], ["Pa", "Pb"], "N")
         if t == RO - 1:
+            batch("v", [code(role(t, sd, j), T.Pe[:, blk(sd, j):blk(sd, j) + 64]) for sd in (0, 1) for j in (0, 1)],
+                  ["Pe"], "N")
             op("v", cp(T.o16[:], N[:]), ["N"], ["o16"])
         else:
+            if t:
+                batch("v", [code(role(t, sd, j), val(sd, j)) for sd in (0, 1) for j in (0, 1)], ka + kb, "N")
             calls = []
             for r in range(8):
                 c7, r4, tb = r >> 2, (r >> 1) & 1, r & 1
@@ -429,33 +469,35 @@ def rank_program(g, core, T, topo):
                     src = N[:, 2 * c7 + tb, r4, :]
                 calls.append(cp(T.o16[:, r:256:8], src))
             batch("v", calls, ["N"], "o16")
-        iin = "Iin%d" % t
         if t == 0:
-            dma(T.ZD[0:128:16, :], T[iin][:], [iin], ["ZD0", "ZDv", "ZDa"])
-            op("a", act(T.X00[:], T.xb0[:], OFF), ["xb0"], ["X00"])
-            op("a", act(T.X01[:], T.xb1[:], OFF), ["xb1"], ["X01"])
-            window(0)
-            window(1)
-            lin([(T.Ps[:, 0:256], [(T.Ip, T.cod[:]), (T.Ip, T.X00[:])]),
-                 (T.Ph[:, 0:256], [(T.Ip, T.Tv[:]), (T.Ip, T.Ta[:])])], ["cod", X0, "Tv", "Ta"], "Ps")
-            wr["Ph"] = dict(wr["Ps"])
-            op("v", ts(T.ti[:], T.Ph[:, 0:256], 0.25 - LIFT, None, A.add), ["Ph"], ["ti"])
-            op("v", ts(T.et[:], T.ti[:], -MID, 1.0 / 4096.0, A.add, A.mult), ["ti"], ["et"])
-            lin([(T.Pe[:, 0:256], [(T.Ip, T.et[:]), (T.Ip, T.X01[:])])], ["et", X1], "Pe")
+            op("g", lambda: g.iota(T.CW[:], [[1, 16], [16, 256]], 0, 0, **small), [], ["CW"])
+            dma(T.ZD[1:128:16, :], T.Jin[:], ["Jin"], ["ZDg", "ZDa", "ZDf"])
+            dma(T.ZD[0:128:16, :], T[iin][:], [iin], ["ZD0"])
+            op("v", ts(T.cod[:], T.c16[:], T.pc[:], 1.0 / 4096.0, A.add, A.mult), ["c16", "pc"], ["cod"])
             place_row(0)
-            inverse_row(0)
+            op("v", tt(T.et[:], T.Tv[:], T.Ta[:], A.add), ["Tv", "Ta"], ["et"])
+            op("v", ts(T.ti[:], T.et[:], 0.25 - LIFT, None, A.add), ["et"], ["ti"])
+            op("v", ts(T.et[:], T.ti[:], -MID, 1.0 / 4096.0, A.add, A.mult), ["ti"], ["et"])
+            op("v", tt(T.emb[:], T.et[:], T.X01[:], A.add), ["et", "X01"], ["emb"])
+            ride(0, 1, "emb")
+            batch("v", [ts(W, T.dg[:], 0.0, sg, A.is_equal, A.mult) for W, sg in ((Ip, 1.0), (Jn, -1.0))], ["dg"], "ident")
+            op("v", tt(T.Gr[:], T[iin][:], T.Jin[:], A.add), [iin, "Jin"], ["Gr"])
+            op("v", ts(T.tk[:], T.Gr[:], 2048.25 - LIFT, None, A.add), ["Gr"], ["tk"])
+            op("v", ts(T.ti[:], T.tk[:], 4095, None, A.bitwise_and), ["tk"], ["ti"])
+            op("v", cp(T.L16[:], T.ti[:]), ["ti"], ["L16"])
         elif t < RO - 1:
-            op("a", act(T.rL[:], T[iin][:], 0.5), [iin], ["rL"])
-            lin([(T.Pl[:, 0:256], [(T.Ip, T[iin][:]), (T.Jn, T.rL[:])])], [iin, "rL"], "Pl")
-        gv(T.AB, T.ZD, T.o16, 0, HV, ["ZD0", "o16"], ["ABa0"])
-        ga(T.AB, T.ZD, T.o16, HV, 256, ["ZD0", "o16"], ABK[1:])
-        dma(T.Hf[:], T.AB[0:128:16, :], ABK, ["Hf"])
+            op("v", tt(T.emb[:], T.Pe[:, 0:256], T["X%d1" % w][:], A.add), ["Pe", "X%d1" % w], ["emb"])
+            ride(w, 1, "emb")
+            if t < 3:
+                place_row(t)
+        gv(T.GO, T.ZD, T.o16, 0, HV, ["ZD0", "ZDg", "o16"], ["GO.v"])
+        ga(T.GO, T.ZD, T.o16, HV, 256, ["ZD0", "ZDg", "o16"], ["GO.a"])
+        dma(T.Hf[:], T.GO[0:128:16, :], gk, ["Hf"])
         if t == 0:
-            op("v", ts(T.tk[:], T.Iin0[:], 2048.25 - LIFT, None, A.add), [iin], ["tk"])
-            op("v", ts(T.tl[:], T.tk[:], 4095, None, A.bitwise_and), ["tk"], ["tl"])
-            op("v", cp(T.L16[:], T.tl[:]), ["tl"], ["L16"])
-        elif t < RO - 1:
+            dma(T.Hg[:], T.GO[1:128:16, :], gk, ["Hg"])
+            rows(1, (0, 1, 2))
+        elif t < RO - 2:
             op("v", code(T.L16[:], T.Pl[:, 0:256], 2048.0), ["Pl"], ["L16"])
-        if t < 2:
-            rows(t + 1)
+        if t == 1:
+            rows(2, (0, 1))
     need("g", top)

@@ -3,13 +3,18 @@ from concourse.mybir import AluOpType, ActivationFunctionType
 
 HOPS = (1, 3, 1, 3, 1, 3)
 RO = len(HOPS)
-NB = 5
-NG = 5
+NB = 4
+NG = 7
+NE = 2
 B0 = 128
-HV = 124
-GV = 128
-IV = 128
-W2 = 10
+HV0, HV1, HV = 88, 128, 128
+GV, GL = 128, 132
+IV = 114
+ZC = 190
+G0 = 4
+W1, G1, W2 = 6, 3, 3
+G2 = 4
+PBE = 1
 NDMA = 76
 
 F, I, U, B = "float32", "int32", "uint16", "bfloat16"
@@ -23,34 +28,36 @@ SCRATCH = {
     "m0": ("sbuf", [128, 1], F), "m1": ("sbuf", [128, 1], F), "pc": ("sbuf", [128, 1], F),
     "Wp": ("sbuf", [128, 144], B), "Wn": ("sbuf", [128, 144], B),
     "dg": ("sbuf", [128, 128], F), "Ip": ("sbuf", [128, 128], F), "Jn": ("sbuf", [128, 128], B),
+    "Jp": ("sbuf", [128, 128], B),
     "Sel": ("sbuf", [128, 4, 128], F),
-    "rH": ("sbuf", [128, 2, 4, 32], B), "Hf": ("sbuf", [128, 2, 4, 32], F), "Hg": ("sbuf", [128, 2, 4, 32], F),
+    "rH": ("sbuf", [128, 2, 4, 32], B), "Hf": ("sbuf", [128, 2, 4, 32], F), "Hin": ("sbuf", [128, 2, 4, 32], F),
+    "Hv": ("sbuf", [128, 2, 4, 32], F), "Ha": ("sbuf", [128, 2, 4, 32], F),
     "ra": ("sbuf", [128, 128], B), "rb": ("sbuf", [128, 128], B),
     "Ea": ("sbuf", [128, 128], F), "Eb": ("sbuf", [128, 128], F),
 }
 for _n in ("a0", "b0", "da", "db", "ea", "eb"):
     SCRATCH[_n] = ("sbuf", [128, 64], F)
-for _n in ("Gr", "zero", "c16", "cod", "st", "emb", "et", "Tv", "Ta", "Jin", "Kin",
-           "X00", "X01", "X10", "X11", "X12", "X20", "X21"):
+for _n in ("Gr", "zero", "c16", "cod", "st", "emb", "et", "Tv", "Ta", "Kin",
+           "X10", "X11", "X12", "X20", "X21"):
     SCRATCH[_n] = ("sbuf", [128, 256], F)
-for _n in ("rE", "rL"):
+for _n in ("rE", "rL", "X00", "X01"):
     SCRATCH[_n] = ("sbuf", [128, 256], B)
 for _n in ("ti", "tk"):
     SCRATCH[_n] = ("sbuf", [128, 256], I)
-for _n in ("G16", "H16", "o16", "L16"):
+for _n in ("G16", "H16", "o16", "L16", "Oout", "Oin"):
     SCRATCH[_n] = ("sbuf", [128, 256], U)
 for _n in ("D", "Pa", "Pb", "Pc", "Pe", "Pk", "Pl", "Ph"):
     SCRATCH[_n] = ("psum", [128, 512], F)
 for _t in range(RO):
-    SCRATCH["N%d" % _t] = ("sbuf", [128, 2 ** (6 - _t), 2, 2 ** (_t + 1)], U if _t else F)
+    SCRATCH["N%d" % _t] = ("sbuf", [128, 2 ** (6 - _t), 2, 2 ** (_t + 1)], U if _t == RO - 1 else F)
     SCRATCH["B%d" % _t] = ("sbuf", [128, 2 ** (7 - _t), 2, 2 ** _t] if _t else [128, 128, 2], F)
     SCRATCH["Bout%d" % _t] = ("sbuf", [128, 256], U)
     SCRATCH["Bin%d" % _t] = ("sbuf", [128, 256], U)
-    SCRATCH["Iin%d" % _t] = ("sbuf", [128, 256], F)
+    SCRATCH["Iin%d" % _t] = ("sbuf", [128, 256], F if _t else U)
     if _t:
         SCRATCH["Iex%d" % _t] = ("sbuf", [128, 256], F)
 
-SEMAPHORES = (["cv", "ca", "cp", "cg", "sent", "j0", "kin"] + ["d%d" % _i for _i in range(NDMA)]
+SEMAPHORES = (["cv", "ca", "cp", "cg", "sent", "oin", "hin", "kin"] + ["d%d" % _i for _i in range(NDMA)]
               + ["b%d_%d" % (_t, _h) for _t in range(RO) for _h in range(2)] + ["i%d" % _t for _t in range(RO)])
 
 OFF = 192.0
@@ -65,10 +72,14 @@ def bits(engines):
     return m
 
 
+def part(tile, half):
+    return tile[:, half] if len(tile.shape) > 2 else tile[:, 128 * half:128 * half + 128]
+
+
 def helpers(core, T, topo):
     r = T.rank_of(core)
     n = len(T.cores)
-    dsts = [T.cores[(r + h) % n] for h in set(HOPS)]
+    dsts = [T.cores[(r + h) % n] for h in HOPS + (-HOPS[0], HOPS[-2] + HOPS[-1])]
     ok = [c for c in topo.cores_of(core) if T.rank_of(c) is None and all(topo.may_write(c, d) for d in dsts)]
     ok.sort(key=lambda c: (topo.die(c) != topo.die(core), c))
     return ok[:2]
@@ -78,16 +89,23 @@ def helper_program(g, core, owner, half, T, topo):
     r = T.rank_of(owner)
     n = len(T.cores)
     got = len(topo.engines(owner, core)) // 2
-    cols = slice(128 * half, 128 * half + 128)
-    total = 0
+    steps = [("Oin", "oin", "Oin", "oin", -HOPS[0])]
     for t in range(RO):
-        dst = T.cores[(r + HOPS[t]) % n]
+        inv, lst = ("Iin%d" % t, "i%d" % t), ("Bin%d" % t, "b%d_%d" % (t, half))
+        if t:
+            steps.append(inv + inv + (HOPS[t],))
+        if t == RO - 2:
+            steps.append(inv + ("Kin", "kin", HOPS[-2] + HOPS[-1]))
+        steps.append(lst + lst + (HOPS[t],))
+        if t == 0:
+            steps += [inv + inv + (HOPS[0],), ("Hin", "hin", "Hin", "hin", HOPS[0])]
+    total = 0
+    for buf, sem, land, lsem, hop in steps:
+        dst = T.cores[(r + hop) % n]
         rid, pid = topo.addr(dst, core)
-        tiles = [("Iin%d" % t, "i%d" % t), ("Bin%d" % t, "b%d_%d" % (t, half))]
-        for buf, sem in ([] if t else [("Jin", "j0")]) + tiles:
-            g.wait_ge(T.sem[sem], got)
-            g.remote_dma(T[buf][:, cols], T[buf][:, cols], T.sem[sem], T.sem.sent, pid, rid, topo.mask(core, dst))
-            total += len(topo.engines(core, dst))
+        g.wait_ge(T.sem[sem], got)
+        g.remote_dma(part(T[land], half), part(T[buf], half), T.sem[lsem], T.sem.sent, pid, rid, topo.mask(core, dst))
+        total += len(topo.engines(core, dst))
     g.wait_ge(T.sem.sent, total)
 
 
@@ -150,16 +168,16 @@ def rank_program(g, core, T, topo):
 
     hs = helpers(core, T, topo)
 
-    def send(src, land, sems, reads):
+    def send(srcs, land, sems, reads):
         order("g", reads, [])
         tr = []
         for h in range(2):
             e = topo.engines(core, hs[h])
             e = e[h * len(e) // 2:(h + 1) * len(e) // 2]
             rid, pid = topo.addr(hs[h], core)
-            cols = slice(128 * h, 128 * h + 128)
             tr.append(RemoteDMATransfer(dst_ids=[DstId(rid=rid, pnc=pid)], dma_engine_mask=bits(e),
-                                        remote_sem=T.sem[sems[h]], src=src[:, cols], dst=land[:, cols]))
+                                        remote_sem=T.sem[sems[h]], srcs=[part(x, h) for x in srcs],
+                                        dsts=[part(land, h)], alu_op=1 if len(srcs) > 1 else 0))
             top["sent"] += len(e)
         g.remote_dma_fused(tr, local_sem=T.sem.sent)
 
@@ -168,12 +186,13 @@ def rank_program(g, core, T, topo):
         top[sem] = count
 
     far = HOPS[-2] + HOPS[-1]
-    lands("Kin", "kin", len(topo.engines(T.cores[(rank - far) % n], core)))
+    lands("Kin", "kin", sum(len(topo.engines(h, core)) for h in helpers(T.cores[(rank - far) % n], T, topo)))
     for t in range(RO):
         cnt = [len(topo.engines(h, core)) for h in helpers(T.cores[(rank - HOPS[t]) % n], T, topo)]
         lands("Iin%d" % t, "i%d" % t, sum(cnt))
         if t == 0:
-            lands("Jin", "j0", sum(cnt))
+            lands("Hin", "hin", sum(cnt))
+            lands("Oin", "oin", sum(len(topo.engines(h, core)) for h in helpers(T.cores[(rank + HOPS[0]) % n], T, topo)))
         for h in range(2):
             lands("Bin%d_%d" % (t, h), "b%d_%d" % (t, h), cnt[h])
 
@@ -204,14 +223,15 @@ def rank_program(g, core, T, topo):
     def ga(out, win, lst, a, b, reads, keys):
         op("a", act(out[:, 16 * a:16 * b], win[:].indirect(lst[:, a:b])), reads, keys)
 
-    def lin(groups, reads, key):
+    def lin(groups, reads, key, begin=True, end=True):
         calls = []
         for out, terms in groups:
             for i, (W, x) in enumerate(terms):
-                calls.append(lambda out=out, W=W, x=x, a=(i == 0), z=(i == len(terms) - 1): g.tensor.matmul(out, W, x, a, z))
+                a, z = begin and i == 0, end and i == len(terms) - 1
+                calls.append(lambda out=out, W=W, x=x, a=a, z=z: g.tensor.matmul(out, W, x, a, z))
         batch("p", calls, reads + ["ident"], key)
 
-    Ip, Jn = T.Ip[:], T.Jn[:]
+    Ip, Jn, Jp = T.Ip[:], T.Jn[:], T.Jp[:]
 
     def role(t, side, j):
         return T["N%d" % t][:, :, side, j::2] if t else T.N0[:, :, side, j]
@@ -232,14 +252,32 @@ def rank_program(g, core, T, topo):
             op("p", lambda: g.tensor.matmul(T.D[:, 0:64], W[:, 16 - P:144 - P], rhs, st, fin),
                reads + ["Wp", "Wn"], ["D"] if st else [], [] if st else ["D"])
 
+    def entry_list(t, reads):
+        N, calls = T["N%d" % t], []
+        for r in range(8):
+            c7, r4, tb = r >> 2, (r >> 1) & 1, r & 1
+            if t <= 3:
+                sp = 2 ** (4 - t)
+                h0 = (2 * c7 + r4) * sp
+                src = N[:, h0 + tb:h0 + sp:2, :, :] if t < 3 else N[:, h0 + tb, :, :]
+            else:
+                src = N[:, 2 * c7 + tb, r4, :]
+            calls.append(code(T.o16[:, r:256:8], src) if t else cp(T.Oout[:, r:256:8], src))
+        batch("v", calls, reads, "o16")
+
     done = [0, 0, 0]
 
-    def window(w, upto):
+    def window(w, upto, q="a"):
         Vw = T["V%d" % w]
         for u in range(done[w], upto):
             run, step = slice(256 * u, 256 * u + 256), slice(u, 4096, 16)
             out, in_ = ((run, run), (step, run), (run, step))[w]
-            op("a", act(Vw[:, out], T.xs[:, in_], OFF), ["xs"], [] if u else ["V%d" % w], ["V%d" % w] if u else [])
+            if q == "a":
+                call = act(Vw[:, out], T.xs[:, in_])
+            else:
+                call = lambda: g.affine_select(Vw[:, out], T.xs[:, in_], [[0, 256]], A.is_ge, 0.0, 0, 0)
+            wr.setdefault("V%d" % w, {})
+            op(q, call, ["xs"], [], ["V%d" % w])
         done[w] = upto
 
     def rows(w, ps):
@@ -250,11 +288,6 @@ def rank_program(g, core, T, topo):
         Vn = "V%d" % w
         dma(T[Vn][p:128:16, :], T[tile][:], [tile, Vn, "X%d%d" % (w, p)], ["%s.%d" % (Vn, p)])
 
-    def place_row(w):
-        op("v", tt(T.st[:], T.cod[:], T["X%d0" % w][:], A.add), ["cod", "X%d0" % w], ["st"])
-        ride(w, 0, "st")
-
-    NV = 16 * NB
     small = dict(allow_small_or_imprecise_dtypes=True)
     dma(T.G[:], T.o[:], [], ["G"])
     op("g", lambda: g.iota(T.ZD[:, 0:256], [[16, 128], [2048, 2]], int(LIFT), 0, **small), [], ["ZD0"])
@@ -262,12 +295,12 @@ def rank_program(g, core, T, topo):
     op("g", lambda: g.iota(T.dg[:], [[1, 128]], 0, -1, **small), [], ["dg"])
     op("g", lambda: g.iota(T.ZD[:, 256 * NB:256 * (NB + NG)], [[1, NG], [16, 128], [2048, 2]], int(LIFT) + NB, 0, **small),
        [], ["ZDg"])
-    op("g", lambda: g.iota(T.c16[:], [[16, 256]], 0, 0, **small), [], ["c16"])
-    op("g", lambda: g.iota(T.ZD[:, 256:256 * NB], [[0, 256 * (NB - 1)]], 0, 0, **small), [], ["ZDf"])
     op("v", lambda: V.memset(T.zero[:], 0.0), [], ["zero"])
     dma(T.Z[0:128:16, :], T.zero[:], ["zero"], ["Z.v"])
     dma(T.GO[0:128:16, :], T.zero[:], ["zero"], ["GO.a"])
     dma(T.xs[:], T.x[:], [], ["xs"])
+    dma(T.X00[:], T.x[0:128:16, :], [], ["X00"])
+    dma(T.X01[:], T.x[1:128:16, :], [], ["X01"])
     batch("a", [act(T.ZD[:, 256 * P:256 * P + 256], T.ZD[:, 0:256], P, ACT.Silu) for P in range(NB + NG, 16)],
           ["ZD0"], "ZDa")
     op("v", lambda: V.memset(T.Wp[:], 0.0), [], ["Wp"])
@@ -278,12 +311,13 @@ def rank_program(g, core, T, topo):
     op("v", ts(T.pk[:], T.pi[:], 15, None, A.bitwise_and), ["pi"], ["pk"])
     op("v", cp(T.m1[:], T.pj[:]), ["pj"], ["m1"])
     op("v", ts(T.m0[:], T.pj[:], -1.0, 1.0, A.mult, A.add), ["pj"], ["m0"])
-    op("v", ts(T.pc[:], T.pk[:], -MID, None, A.add), ["pk"], ["pc"])
+    op("v", ts(T.pc[:], T.pk[:], 4096.0 * OFF - MID, None, A.add), ["pk"], ["pc"])
     batch("v", [ts(T.Sel[:, 2 * q + c, :], T.dg[:], 16.0 * (c - q), (T.m0, T.m1)[q][:], A.is_equal, A.mult)
                 for q in (0, 1) for c in (0, 1)], ["dg", "m0", "m1"], "ident")
     op("v", cp(T.G16[:], T.G[:]), ["G"], ["G16"])
-    op("a", lambda: S.activation(T.GO[:].indirect(T.G16[:, NV:256]), T.ZD[:, 16 * NV:4096], ACT.Silu),
-       ["G16", "ZDa", "ZDg"], ["GO.a"])
+    for a, b, key in ((NB + NG, 16, "ZDa"), (NB, NB + NG, "ZDg")):
+        op("a", lambda: S.activation(T.GO[:].indirect(T.G16[:, 16 * a:16 * b]), T.ZD[:, 256 * a:256 * b], ACT.Silu),
+           ["G16", key], ["GO.a"])
     batch("v", [cp(T.Gr[:, 32 * (u & 7) + 16 * (u >> 3):32 * (u & 7) + 16 * (u >> 3) + 16], T.G[:, u:256:16])
                 for u in range(16)], ["G"], "Gr")
     batch("v", [(lambda u=u: V.transpose(T.Gt[:, u, :], T.Gr[:, 32 * u:32 * u + 32])) for u in range(8)], ["Gr"], "Gt")
@@ -292,10 +326,14 @@ def rank_program(g, core, T, topo):
     for P in range(NB):
         op("v", ts(T.Z[:].indirect(T.G16[:, 16 * P:16 * P + 16]), T.ZD[:, 0:256], 1.0, float(P), A.mult, A.add),
            ["G16", "ZD0"], ["Z.v"])
+        if P == NE - 1:
+            op("v", cp(T.N0[:], T.Pa[:, 0:256]), ["Pa"], ["N"])
+            entry_list(0, ["N"])
+            send([T.Oout], T.Oin, ["oin", "oin"], ["o16"])
+            op("g", lambda: g.iota(T.ZD[:, 256:256 * NB], [[0, 256 * (NB - 1)]], 0, 0, **small), [], ["ZDf"])
+            op("g", lambda: g.iota(T.c16[:], [[16, 256]], 0, 0, **small), [], ["c16"])
     dma(T.Tv[:], T.Z[0:128:16, :], ["Z.v"], ["Tv"])
-    send(T.Tv, T.Jin, ["j0", "j0"], ["Tv"])
     dma(T.Ta[:], T.GO[0:128:16, :], ["GO.a"], ["Ta"])
-    send(T.Ta, T.Iin0, ["i0", "i0"], ["Ta"])
     rd["Z.a"], rd["GO.v"] = dict(rd["Z.v"]), dict(rd["GO.a"])
     batch("v", [cp(T.H16[:, blk(sd, j):blk(sd, j) + 64], T.Pa[:, 2 * sd + j:256:4]) for sd in (1, 0) for j in (0, 1)],
           ["Pa"], "H16")
@@ -310,10 +348,13 @@ def rank_program(g, core, T, topo):
             wk = [Vn] + ["%s.%d" % (Vn, p) for p in range(3)]
             b0, b1 = "Bin%d_0" % (t - 1), "Bin%d_1" % (t - 1)
             Bin = T["Bin%d" % (t - 1)]
-            gv(T.Z, T[Vn], Bin, 0, GV, wk + [b0] + ([b1] if GV > 128 else []), ["Z.v"])
-            ga(T.Z, T[Vn], Bin, GV, 256, wk + [b1] + ([b0] if GV < 128 else []), ["Z.a"])
+            mid, cut = (GL, ZC) if t >= RO - 1 else (GV, 256)
+            gv(T.Z, T[Vn], Bin, 0, mid, wk + [b0] + ([b1] if mid > 128 else []), ["Z.v"])
+            ga(T.Z, T[Vn], Bin, mid, cut, wk + [b1] + ([b0] if mid < 128 else []), ["Z.a"])
             if t > 1:
                 op("a", act(T.rH[:], T.Hf[:]), ["Hf"], ["rH"])
+            if cut < 256:
+                op("a", act(T.Z[:, 16 * cut:4096], T[Vn][:].indirect(Bin[:, cut:256])), wk + [b1], [], ["Z.a"])
             if t == RO:
                 lin([(T.Ph[:, 0:256], [(Ip, T.Hf[:]), (Jn, T.rH[:])])], ["Hf", "rH"], "Ph")
                 op("v", code(T.H16[:], T.Ph[:, 0:256]), ["Ph"], ["H16"])
@@ -321,26 +362,30 @@ def rank_program(g, core, T, topo):
                 ga(T.GO, T.Z, T.H16, 128, 256, zk + ["H16"], ["GO.a"])
                 dma(T.yo[:], T.GO[0:128:16, :], gk, [])
                 break
-            W, other = (Jn, "rH") if t > 1 else (Ip, "Hg")
-            lin([(T.Ph[:, 64 * z:64 * z + 64], [(Ip, T.Hf[:, :, z, :]), (W, T[other][:, :, z, :])]) for z in range(4)],
-                ["Hf", other], "Ph")
+            if t > 1:
+                lin([(T.Ph[:, 64 * z:64 * z + 64], [(Ip, T.Hf[:, :, z, :]), (Jn, T.rH[:, :, z, :])]) for z in range(4)],
+                    ["Hf", "rH"], "Ph")
+            if t == 2:
+                rows(2, (0, 1))
             if t < RO - 1:
-                gv(T.GO, T.Z, T.L16, 0, IV, zk + ["L16"], ["GO.v"])
-                ga(T.GO, T.Z, T.L16, IV, 256, zk + ["L16"], ["GO.a"])
+                lin([(T.Pe[:, 0:256], [(Ip if w else Jp, T["X%d1" % w][:])])], ["X%d1" % w], "Pe", end=False)
+            if t == RO - 2:
+                lin([(T.Pk[:, 0:256], [(Ip, T.X12[:])])], ["X12"], "Pk", end=False)
+            if t < RO - 1:
+                lk = "L16" if t > 1 else "Iin0"
+                gv(T.GO, T.Z, T[lk], 0, IV, zk + [lk], ["GO.v"])
+                ga(T.GO, T.Z, T[lk], IV, 256, zk + [lk], ["GO.a"])
                 dma(T[iex][:], T.GO[1:128:16, :], gk, ["Iex"])
             else:
                 dma(T[iex][:], T.Z[1:128:16, :], zk, ["Iex"])
-            send(T[iex], T[iin], ["i%d" % t] * 2, ["Iex"])
-            if t == RO - 2:
-                dst = T.cores[(rank + far) % n]
-                rid, pid = topo.addr(dst, core)
-                g.remote_dma(T.Kin[:], T[iex][:], T.sem.kin, T.sem.sent, pid, rid, topo.mask(core, dst))
-                top["sent"] += len(topo.engines(core, dst))
+            send([T[iex]], T[iin], ["i%d" % t] * 2, ["Iex"])
+            if t == 1:
+                window(2, G2 + 5, "g")
             if t > 1:
                 calls = [code(T.H16[:, z:256:4], T.Ph[:, 64 * z:64 * z + 64]) for z in range(4)]
             else:
-                calls = [ts(T.H16[:, z:256:4], T.Ph[:, 64 * z:64 * z + 64], 0.25 - LIFT, None, A.add) for z in range(4)]
-            batch("v", calls, ["Ph"], "H16")
+                calls = [ts(T.H16[:, z:256:4], T.Hin[:, :, z, :], 0.25 - LIFT, None, A.add) for z in range(4)]
+            batch("v", calls, ["Ph" if t > 1 else "Hin"], "H16")
             hk = zk + ["H16"]
 
             def piece(eng, side, j, h, key):
@@ -362,6 +407,13 @@ def rank_program(g, core, T, topo):
             def whole(r, E, j):
                 op("a", act(T[r][:, (j0, j1)[j]], T[E][:, (j0, j1)[j]]), ["%s%d" % (E, j)], ["%s%d" % (r, j)])
 
+            kk = []
+
+            def second(sd, j):
+                if t == RO - 1:
+                    kk.append("K%d%d" % (sd, j))
+                    fold(T.et[:, blk(sd, j):blk(sd, j) + 64], 2, sd, j, kk[-1])
+
             piece(gv, 1, 0, 0, "b00")
             piece(ga, 1, 1, 0, "b10")
             piece(ga, 1, 0, 1, "b01")
@@ -370,13 +422,12 @@ def rank_program(g, core, T, topo):
             fold(T.Eb[:, j1], 0, 1, 1, "Eb1")
             piece(ga, 0, 0, 0, "a0r")
             fold(T.Ea[:, j0], 0, 0, 0, "Ea0")
+            second(1, 0)
+            second(1, 1)
             piece(ga, 0, 1, 0, "a1r")
             fold(T.Ea[:, j1], 0, 0, 1, "Ea1")
-            kk = []
-            if t == RO - 1:
-                for sd, j in ((1, 0), (1, 1), (0, 0), (0, 1)):
-                    kk.append("K%d%d" % (sd, j))
-                    fold(T.et[:, blk(sd, j):blk(sd, j) + 64], 2, sd, j, kk[-1])
+            second(0, 0)
+            second(0, 1)
             whole("rb", "Eb", 1)
             whole("rb", "Eb", 0)
             whole("ra", "Ea", 0)
@@ -387,32 +438,26 @@ def rank_program(g, core, T, topo):
             fused("M2", 0, 1, 0, 8)
             fused("M1", 0, 0, 8, 16)
             fused("M2", 1, 0, 8, 16)
+            if PBE:
+                lin([(T.Pb[:, j0], [(Ip, T.Eb[:, j1]), (Jn, T.rb[:, j1])])], ["Eb1", "rb1"], "Pb")
             fused("M1", 1, 1, 8, 16)
-            lin([(T.Pb[:, j0], [(Ip, T.Eb[:, j1]), (Jn, T.rb[:, j1])])], ["Eb1", "rb1"], "Pb")
+            if not PBE:
+                lin([(T.Pb[:, j0], [(Ip, T.Eb[:, j1]), (Jn, T.rb[:, j1])])], ["Eb1", "rb1"], "Pb")
             fused("M2", 0, 1, 8, 13)
             fused("M2", 0, 1, 13, 16, True)
             lin([(T.Pa[:, j0], [(Ip, T.Ea[:, j1]), (Jn, T.ra[:, j1])])], ["Ea1", "ra1"], "Pa")
-            op("v", tt(T.b0[:], T.Eb[:, j0], T.rb[:, j0], A.subtract), ["Eb0", "rb0"], ["b0"])
-            op("v", tt(T.a0[:], T.Ea[:, j0], T.ra[:, j0], A.subtract), ["Ea0", "ra0"], ["a0"])
-            op("v", tt(T.db[:], T.Pb[:, j0], T.b0[:], A.subtract), ["Pb", "b0"], ["db"])
-            dma(T.ZD[0:128:16, :], T[iin][:], [iin], ["ZD0"])
+            a0, b0 = (role(t, 0, 0), role(t, 1, 0)) if t < RO - 1 else (T.a0[:], T.b0[:])
+            op("v", tt(b0, T.Eb[:, j0], T.rb[:, j0], A.subtract), ["Eb0", "rb0"], ["b0"])
+            op("v", tt(a0, T.Ea[:, j0], T.ra[:, j0], A.subtract), ["Ea0", "ra0"], ["a0"])
+            op("v", tt(T.db[:], T.Pb[:, j0], b0, A.subtract), ["Pb", "b0"], ["db"])
+            dma(T.ZD[0:128:16, :], T[iin][:], [iin], ["ZD0", "ZDg"])
             if t < RO - 1:
                 op("a", act(T.rE[:], T[iex][:]), ["Iex"], ["rE"])
-                lin([(T.Pe[:, 0:256], [(Ip, T[iex][:]), (Jn, T.rE[:])])], ["Iex", "rE"], "Pe")
+                lin([(T.Pe[:, 0:256], [(Ip, T[iex][:]), (Jn, T.rE[:])])], ["Iex", "rE"], "Pe", begin=False)
             else:
                 op("a", act(T.rE[:], T.et[:]), kk, ["rE"])
                 lin([(T.Pe[:, 0:256], [(Ip, T.et[:]), (Jn, T.rE[:])])], kk + ["rE"], "Pe")
-            if t < RO - 2:
-                op("a", act(T.rL[:], T[iin][:], 0.5), [iin], ["rL"])
-                lin([(T.Pl[:, 0:256], [(Ip, T[iin][:]), (Jn, T.rL[:])])], [iin, "rL"], "Pl")
-                if t == 1:
-                    window(2, 16)
-            elif t == RO - 2:
-                op("a", act(T.rL[:], T.Kin[:], 0.5), ["Kin"], ["rL"])
-                lin([(T.Pk[:, 0:256], [(Ip, T.Kin[:]), (Jn, T.rL[:]), (Ip, T.X12[:])])], ["Kin", "rL", "X12"], "Pk")
-                op("a", act(T.st[:], T.Pk[:, 0:256], 0.5), ["Pk"], ["st"])
-                ride(w, 2, "st")
-            val = lambda sd, j: ((T.a0[:], T.Pa[:, j0]), (T.b0[:], T.Pb[:, j0]))[sd][j]
+            val = lambda sd, j: ((a0, T.Pa[:, j0]), (b0, T.Pb[:, j0]))[sd][j]
             ka, kb = ["Pa", "a0"], ["Pb", "b0"]
         else:
             for eng, a, b in (("v", 0, B0), ("a", B0, 128)):
@@ -422,34 +467,36 @@ def rank_program(g, core, T, topo):
                         c = blk(1, j) - 64 * j
                         src, out = T.xs[:].indirect(T.H16[:, c + lo:c + hi]), T.bb[:, 16 * lo:16 * hi]
                         op(eng, cp(out, src) if eng == "v" else act(out, src), ["xs", "H16"], ["bb%s%d" % (eng, j)])
+            window(0, 1)
+            window(0, 1 + G0, "g")
             window(0, 16)
-            rows(0, (0, 1))
-            window(1, 16)
-            window(2, W2)
+            window(1, W1)
             for M, j, jb in (("M1", 0, 0), ("M2", 1, 0), ("M1", 1, 1), ("M2", 0, 1)):
                 keys = ["%s.%d.%d" % (M, j, p0) for p0 in (0, 8, 13)]
                 op("v", tt(T[M][:, 1024 * j:1024 * j + 1024], T.xs[:].indirect(T.H16[:, blk(0, j):blk(0, j) + 64]),
                            T.bb[:, 1024 * jb:1024 * jb + 1024], A.max), ["xs", "H16", "bbv%d" % jb, "bba%d" % jb], keys)
                 sums([(P, T.Wp if M == "M1" else T.Wn, T[M][:, 1024 * j + P:1024 * j + 1024:16]) for P in range(16)],
                      keys, (M, j) == ("M2", 0))
-            op("v", cp(T.N0[:], T.Pa[:, 0:256]), ["Pa"], ["N"])
+            op("v", tt(T.Gr[:], T.Tv[:], T.Ta[:], A.add), ["Tv", "Ta"], ["Gr"])
+            dma(T.ZD[0:128:16, :], T.Gr[:], ["Gr"], ["ZD0", "ZDg", "ZDa", "ZDf"])
             op("v", tt(T.db[:], role(0, 1, 1), role(0, 1, 0), A.subtract), ["N"], ["db"])
             op("v", tt(T.da[:], role(0, 0, 1), role(0, 0, 0), A.subtract), ["N"], ["da"])
+            op("v", ts(T.cod[:], T.c16[:], T.pc[:], 1.0 / 4096.0, A.add, A.mult), ["c16", "pc"], ["cod"])
             val = lambda sd, j: role(0, sd, j)
             ka, kb = ["N"], ["N"]
         s = T.Pc[:, j0]
         op("v", ts(s, T.D[:, j0], 0.0, None, A.is_gt), ["D"], ["s"])
+        op("v", tt(T.eb[:], T.db[:], s, A.mult), ["db", "s"], ["eb"])
         if t:
             op("v", tt(T.da[:], val(0, 1), val(0, 0), A.subtract), ka, ["da"])
-        op("v", tt(T.eb[:], T.db[:], s, A.mult), ["db", "s"], ["eb"])
+        op("v", tt(brole(t, 0, 0), val(1, 0), T.eb[:], A.add), kb + ["eb"], ["Bb"])
         op("v", tt(T.ea[:], T.da[:], s, A.mult), ["da", "s"], ["ea"])
-        batch("v", [tt(brole(t, 0, 0), val(1, 0), T.eb[:], A.add), tt(brole(t, 0, 1), val(1, 1), T.eb[:], A.subtract)],
-              kb + ["eb"], "Bb")
+        op("v", tt(brole(t, 0, 1), val(1, 1), T.eb[:], A.subtract), kb + ["eb"], [], ["Bb"])
         batch("v", [tt(brole(t, 1, 0), val(0, 1), T.ea[:], A.subtract), tt(brole(t, 1, 1), val(0, 0), T.ea[:], A.add)],
               ka + ["ea"], "Ba")
         Bt, Bo = T["B%d" % t][:], T["Bout%d" % t][:]
         op("v", code(Bo, Bt) if t else cp(Bo, Bt), ["Ba", "Bb"], ["Bout"])
-        send(T["Bout%d" % t], T["Bin%d" % t], ["b%d_0" % t, "b%d_1" % t], ["Bout"])
+        send([T["Bout%d" % t]], T["Bin%d" % t], ["b%d_0" % t, "b%d_1" % t], ["Bout"])
         N = T["N%d" % t]
         if t == RO - 1:
             batch("v", [code(role(t, sd, j), T.Pe[:, blk(sd, j):blk(sd, j) + 64]) for sd in (0, 1) for j in (0, 1)],
@@ -457,47 +504,57 @@ def rank_program(g, core, T, topo):
             op("v", cp(T.o16[:], N[:]), ["N"], ["o16"])
         else:
             if t:
-                batch("v", [code(role(t, sd, j), val(sd, j)) for sd in (0, 1) for j in (0, 1)], ka + kb, "N")
-            calls = []
-            for r in range(8):
-                c7, r4, tb = r >> 2, (r >> 1) & 1, r & 1
-                if t <= 3:
-                    sp = 2 ** (4 - t)
-                    h0 = (2 * c7 + r4) * sp
-                    src = N[:, h0 + tb:h0 + sp:2, :, :] if t < 3 else N[:, h0 + tb, :, :]
-                else:
-                    src = N[:, 2 * c7 + tb, r4, :]
-                calls.append(cp(T.o16[:, r:256:8], src))
-            batch("v", calls, ["N"], "o16")
+                batch("a", [act(role(t, sd, 1), val(sd, 1)) for sd in (1, 0)], ka + kb + ["Ba", "Bb"], "N")
+                entry_list(t, ["N"] + ka + kb)
         if t == 0:
-            op("g", lambda: g.iota(T.CW[:], [[1, 16], [16, 256]], 0, 0, **small), [], ["CW"])
-            dma(T.ZD[1:128:16, :], T.Jin[:], ["Jin"], ["ZDg", "ZDa", "ZDf"])
-            dma(T.ZD[0:128:16, :], T[iin][:], [iin], ["ZD0"])
-            op("v", ts(T.cod[:], T.c16[:], T.pc[:], 1.0 / 4096.0, A.add, A.mult), ["c16", "pc"], ["cod"])
-            place_row(0)
-            op("v", tt(T.et[:], T.Tv[:], T.Ta[:], A.add), ["Tv", "Ta"], ["et"])
-            op("v", ts(T.ti[:], T.et[:], 0.25 - LIFT, None, A.add), ["et"], ["ti"])
-            op("v", ts(T.et[:], T.ti[:], -MID, 1.0 / 4096.0, A.add, A.mult), ["ti"], ["et"])
+            op("v", ts(T.tk[:], T.Gr[:], 2048.25 - LIFT, None, A.add), ["Gr"], ["tk"])
+            op("v", tt(T.st[:], T.cod[:], T.X00[:], A.add), ["cod", "X00"], ["st"])
+            ride(0, 0, "st")
+            op("v", ts(T.ti[:], T.tk[:], 4095, None, A.bitwise_and), ["tk"], ["ti"])
+            op("v", ts(T.et[:], T.tk[:], 4096.0 * OFF - MID - 2048.0, 1.0 / 4096.0, A.add, A.mult), ["tk"], ["et"])
+            op("v", cp(T.G16[:], T.ti[:]), ["ti"], ["G16"])
+            send([T.G16], T.Iin0, ["i0", "i0"], ["G16"])
             op("v", tt(T.emb[:], T.et[:], T.X01[:], A.add), ["et", "X01"], ["emb"])
             ride(0, 1, "emb")
-            batch("v", [ts(W, T.dg[:], 0.0, sg, A.is_equal, A.mult) for W, sg in ((Ip, 1.0), (Jn, -1.0))], ["dg"], "ident")
-            op("v", tt(T.Gr[:], T[iin][:], T.Jin[:], A.add), [iin, "Jin"], ["Gr"])
-            op("v", ts(T.tk[:], T.Gr[:], 2048.25 - LIFT, None, A.add), ["Gr"], ["tk"])
-            op("v", ts(T.ti[:], T.tk[:], 4095, None, A.bitwise_and), ["tk"], ["ti"])
-            op("v", cp(T.L16[:], T.ti[:]), ["ti"], ["L16"])
-        elif t < RO - 1:
-            op("v", tt(T.emb[:], T.Pe[:, 0:256], T["X%d1" % w][:], A.add), ["Pe", "X%d1" % w], ["emb"])
-            ride(w, 1, "emb")
-            if t < 3:
-                place_row(t)
-        gv(T.GO, T.ZD, T.o16, 0, HV, ["ZD0", "ZDg", "o16"], ["GO.v"])
-        ga(T.GO, T.ZD, T.o16, HV, 256, ["ZD0", "ZDg", "o16"], ["GO.a"])
-        dma(T.Hf[:], T.GO[0:128:16, :], gk, ["Hf"])
-        if t == 0:
-            dma(T.Hg[:], T.GO[1:128:16, :], gk, ["Hg"])
-            rows(1, (0, 1, 2))
-        elif t < RO - 2:
-            op("v", code(T.L16[:], T.Pl[:, 0:256], 2048.0), ["Pl"], ["L16"])
+            gv(T.GO, T.ZD, T.Oin, 0, HV0, ["ZD0", "Oin"], ["GO.v"])
+            ga(T.GO, T.ZD, T.Oin, HV0, 256, ["ZD0", "Oin"], ["GO.a"])
+            batch("v", [ts(W, T.dg[:], 0.0, sg, A.is_equal, A.mult) for W, sg in ((Ip, 1.0), (Jn, -1.0), (Jp, 1.0))],
+                  ["dg"], "ident")
+            dma(T.Hv[:], T.GO[0:128:16, :], gk, ["Hv"])
+            window(1, W1 + G1, "g")
+            send([T.Hv], T.Hin, ["hin", "hin"], ["Hv"])
+            window(1, W1 + G1 + W2)
+            window(1, 16, "g")
+            rows(1, (0, 1))
+            window(2, G2, "g")
+            continue
         if t == 1:
-            rows(2, (0, 1))
+            window(2, 16, "g")
+        if t == 2:
+            op("g", lambda: g.iota(T.CW[:], [[1, 16], [16, 256]], 0, 0, **small), [], ["CW"])
+        if t < RO - 1:
+            op("a", act(T.emb[:], T.Pe[:, 0:256], OFF), ["Pe"], ["emb"])
+            ride(w, 1, "emb")
+        if t < 3:
+            op("v", tt(T.st[:], T.cod[:], T["X%d0" % w][:], A.add), ["cod", "X%d0" % w], ["st"])
+            ride(w, 0, "st")
+        if t < RO - 2:
+            op("a", act(T.rL[:], T[iin][:], 0.5), [iin], ["rL"])
+            lin([(T.Pl[:, 0:256], [(Ip, T[iin][:]), (Jn, T.rL[:])])], [iin, "rL"], "Pl")
+        elif t == RO - 2:
+            op("a", act(T.rL[:], T.Kin[:], 0.5), ["Kin"], ["rL"])
+            lin([(T.Pk[:, 0:256], [(Ip, T.Kin[:]), (Jn, T.rL[:])])], ["Kin", "rL"], "Pk", begin=False)
+        if t == 2:
+            rows(1, (2,))
+        hv = HV1 if t == 1 else HV
+        cut = hv + 56 if t == RO - 2 else 256
+        gv(T.GO, T.ZD, T.o16, 0, hv, ["ZD0", "o16"], ["GO.v"])
+        ga(T.GO, T.ZD, T.o16, hv, cut, ["ZD0", "o16"], ["GO.a"])
+        if t == RO - 2:
+            op("a", act(T.st[:], T.Pk[:, 0:256], OFF + 0.5), ["Pk"], ["st"])
+            ride(w, 2, "st")
+            op("a", act(T.GO[:, 16 * cut:4096], T.ZD[:].indirect(T.o16[:, cut:256])), ["ZD0", "o16"], [], ["GO.a"])
+        dma(T.Hf[:], T.GO[0:128:16, :], gk, ["Hf"])
+        if t < RO - 2:
+            op("v", code(T.L16[:], T.Pl[:, 0:256], 2048.0), ["Pl"], ["L16"])
     need("g", top)

from concourse.bass import DstId, RemoteDMATransfer
from concourse.mybir import AluOpType, ActivationFunctionType

HOPS = (1, 3, 1, 3, 1, 3)
RO = len(HOPS)
NB = 4
NG = 7
NE = 2
B0 = 128
HV0, HV1, HV = 88, 128, 128
GV, GL = 128, 132
IV = 114
ZC = 190
G0 = 4
W1, G1, W2 = 6, 3, 3
G2 = 4
PBE = 1
NDMA = 76

F, I, U, B = "float32", "int32", "uint16", "bfloat16"
SCRATCH = {
    "xs": ("sbuf", [128, 4096], B), "V0": ("sbuf", [128, 4096], F), "V1": ("sbuf", [128, 4096], F),
    "V2": ("sbuf", [128, 4096], F), "Z": ("sbuf", [128, 4096], F), "GO": ("sbuf", [128, 4096], F),
    "AB": ("sbuf", [128, 4096], F), "ZD": ("sbuf", [128, 4096], F), "CW": ("sbuf", [128, 4096], F),
    "M1": ("sbuf", [128, 2048], B), "M2": ("sbuf", [128, 2048], B), "bb": ("sbuf", [128, 2048], B),
    "G": ("sbuf", [128, 256], I), "Gt": ("sbuf", [128, 8, 32], F),
    "pi": ("sbuf", [128, 1], I), "pj": ("sbuf", [128, 1], I), "pk": ("sbuf", [128, 1], I),
    "m0": ("sbuf", [128, 1], F), "m1": ("sbuf", [128, 1], F), "pc": ("sbuf", [128, 1], F),
    "Wp": ("sbuf", [128, 144], B), "Wn": ("sbuf", [128, 144], B),
    "dg": ("sbuf", [128, 128], F), "Ip": ("sbuf", [128, 128], F), "Jn": ("sbuf", [128, 128], B),
    "Jp": ("sbuf", [128, 128], B),
    "Sel": ("sbuf", [128, 4, 128], F),
    "rH": ("sbuf", [128, 2, 4, 32], B), "Hf": ("sbuf", [128, 2, 4, 32], F), "Hin": ("sbuf", [128, 2, 4, 32], F),
    "Hv": ("sbuf", [128, 2, 4, 32], F), "Ha": ("sbuf", [128, 2, 4, 32], F),
    "ra": ("sbuf", [128, 128], B), "rb": ("sbuf", [128, 128], B),
    "Ea": ("sbuf", [128, 128], F), "Eb": ("sbuf", [128, 128], F),
}
for _n in ("a0", "b0", "da", "db", "ea", "eb"):
    SCRATCH[_n] = ("sbuf", [128, 64], F)
for _n in ("Gr", "zero", "c16", "cod", "st", "emb", "et", "Tv", "Ta", "Kin",
           "X10", "X11", "X12", "X20", "X21"):
    SCRATCH[_n] = ("sbuf", [128, 256], F)
for _n in ("rE", "rL", "X00", "X01"):
    SCRATCH[_n] = ("sbuf", [128, 256], B)
for _n in ("ti", "tk"):
    SCRATCH[_n] = ("sbuf", [128, 256], I)
for _n in ("G16", "H16", "o16", "L16", "Oout", "Oin"):
    SCRATCH[_n] = ("sbuf", [128, 256], U)
for _n in ("D", "Pa", "Pb", "Pc", "Pe", "Pk", "Pl", "Ph"):
    SCRATCH[_n] = ("psum", [128, 512], F)
for _t in range(RO):
    SCRATCH["N%d" % _t] = ("sbuf", [128, 2 ** (6 - _t), 2, 2 ** (_t + 1)], U if _t == RO - 1 else F)
    SCRATCH["B%d" % _t] = ("sbuf", [128, 2 ** (7 - _t), 2, 2 ** _t] if _t else [128, 128, 2], F)
    SCRATCH["Bout%d" % _t] = ("sbuf", [128, 256], U)
    SCRATCH["Bin%d" % _t] = ("sbuf", [128, 256], U)
    SCRATCH["Iin%d" % _t] = ("sbuf", [128, 256], F if _t else U)
    if _t:
        SCRATCH["Iex%d" % _t] = ("sbuf", [128, 256], F)

SEMAPHORES = (["cv", "ca", "cp", "cg", "sent", "oin", "hin", "kin"] + ["d%d" % _i for _i in range(NDMA)]
              + ["b%d_%d" % (_t, _h) for _t in range(RO) for _h in range(2)] + ["i%d" % _t for _t in range(RO)])

OFF = 192.0
MID = 2047.5
LIFT = 32.0


def bits(engines):
    m = 0
    for e in engines:
        m |= 1 << e
    return m


def part(tile, half):
    return tile[:, half] if len(tile.shape) > 2 else tile[:, 128 * half:128 * half + 128]


def helpers(core, T, topo):
    r = T.rank_of(core)
    n = len(T.cores)
    dsts = [T.cores[(r + h) % n] for h in HOPS + (-HOPS[0], HOPS[-2] + HOPS[-1])]
    ok = [c for c in topo.cores_of(core) if T.rank_of(c) is None and all(topo.may_write(c, d) for d in dsts)]
    ok.sort(key=lambda c: (topo.die(c) != topo.die(core), c))
    return ok[:2]


def helper_program(g, core, owner, half, T, topo):
    r = T.rank_of(owner)
    n = len(T.cores)
    got = len(topo.engines(owner, core)) // 2
    steps = [("Oin", "oin", "Oin", "oin", -HOPS[0])]
    for t in range(RO):
        inv, lst = ("Iin%d" % t, "i%d" % t), ("Bin%d" % t, "b%d_%d" % (t, half))
        if t:
            steps.append(inv + inv + (HOPS[t],))
        if t == RO - 2:
            steps.append(inv + ("Kin", "kin", HOPS[-2] + HOPS[-1]))
        steps.append(lst + lst + (HOPS[t],))
        if t == 0:
            steps += [inv + inv + (HOPS[0],), ("Hin", "hin", "Hin", "hin", HOPS[0])]
    total = 0
    for buf, sem, land, lsem, hop in steps:
        dst = T.cores[(r + hop) % n]
        rid, pid = topo.addr(dst, core)
        g.wait_ge(T.sem[sem], got)
        g.remote_dma(part(T[land], half), part(T[buf], half), T.sem[lsem], T.sem.sent, pid, rid, topo.mask(core, dst))
        total += len(topo.engines(core, dst))
    g.wait_ge(T.sem.sent, total)


def rank_program(g, core, T, topo):
    rank = T.rank_of(core)
    if rank is None:
        for owner in topo.cores_of(core):
            if T.rank_of(owner) is not None:
                hs = helpers(owner, T, topo)
                if core in hs:
                    helper_program(g, core, owner, hs.index(core), T, topo)
        return
    n = len(T.cores)
    A = AluOpType
    ACT = ActivationFunctionType
    Q = {"v": g.vector, "a": g.scalar, "p": g.tensor, "g": g, "s": g.sync}
    seen = {q: {} for q in Q}
    wr, rd, top = {}, {}, {"sent": 0}
    ndma = [0]

    def need(q, toks):
        for sem, val in toks.items():
            if seen[q].get(sem, 0) < val:
                Q[q].wait_ge(T.sem[sem], val)
                seen[q][sem] = val

    def order(q, reads, writes):
        for k in reads:
            need(q, wr.get(k, {}))
        for k in writes:
            need(q, wr.get(k, {}))
            need(q, rd.get(k, {}))

    def note(sem, val, reads, writes, also):
        top[sem] = val
        for k in reads:
            rd.setdefault(k, {})[sem] = val
        for k in writes:
            wr[k] = {sem: val}
            rd[k] = {}
        for k in also:
            wr[k][sem] = val

    def op(q, call, reads, writes, also=()):
        order(q, reads, writes)
        sem = "c" + q
        call().then_inc(T.sem[sem], 1)
        note(sem, top.get(sem, 0) + 1, reads, writes, also)

    def batch(q, calls, reads, key):
        for i, call in enumerate(calls):
            op(q, call, reads, [] if i else [key], [key] if i else [])

    def dma(out, in_, reads, writes):
        order("s", reads, writes)
        sem = "d%d" % ndma[0]
        ndma[0] += 1
        g.sync.dma_start(out, in_).then_inc(T.sem[sem], 16)
        note(sem, 16, reads, writes, ())

    hs = helpers(core, T, topo)

    def send(srcs, land, sems, reads):
        order("g", reads, [])
        tr = []
        for h in range(2):
            e = topo.engines(core, hs[h])
            e = e[h * len(e) // 2:(h + 1) * len(e) // 2]
            rid, pid = topo.addr(hs[h], core)
            tr.append(RemoteDMATransfer(dst_ids=[DstId(rid=rid, pnc=pid)], dma_engine_mask=bits(e),
                                        remote_sem=T.sem[sems[h]], srcs=[part(x, h) for x in srcs],
                                        dsts=[part(land, h)], alu_op=1 if len(srcs) > 1 else 0))
            top["sent"] += len(e)
        g.remote_dma_fused(tr, local_sem=T.sem.sent)

    def lands(key, sem, count):
        wr[key] = {sem: count}
        top[sem] = count

    far = HOPS[-2] + HOPS[-1]
    lands("Kin", "kin", sum(len(topo.engines(h, core)) for h in helpers(T.cores[(rank - far) % n], T, topo)))
    for t in range(RO):
        cnt = [len(topo.engines(h, core)) for h in helpers(T.cores[(rank - HOPS[t]) % n], T, topo)]
        lands("Iin%d" % t, "i%d" % t, sum(cnt))
        if t == 0:
            lands("Hin", "hin", sum(cnt))
            lands("Oin", "oin", sum(len(topo.engines(h, core)) for h in helpers(T.cores[(rank + HOPS[0]) % n], T, topo)))
        for h in range(2):
            lands("Bin%d_%d" % (t, h), "b%d_%d" % (t, h), cnt[h])

    V, S = g.vector, g.scalar

    def ts(out, in_, s1, s2, o1, o2=None):
        if o2 is None:
            return lambda: V.tensor_scalar(out, in_, s1, None, o1)
        return lambda: V.tensor_scalar(out, in_, s1, s2, o1, o2)

    def cp(out, in_):
        return lambda: V.tensor_copy(out, in_)

    def tt(out, a, b, o):
        return lambda: V.tensor_tensor(out, a, b, o)

    def act(out, in_, bias=None, func=None):
        if bias is None:
            return lambda: S.activation(out, in_, func or ACT.Identity)
        return lambda: S.activation(out, in_, func or ACT.Identity, bias=float(bias))

    def code(out, frac, extra=0.0):
        return ts(out, frac, 4096.0, MID + extra, A.mult, A.add)

    def gv(out, win, lst, a, b, reads, keys):
        op("v", cp(out[:, 16 * a:16 * b], win[:].indirect(lst[:, a:b])), reads, keys)

    def ga(out, win, lst, a, b, reads, keys):
        op("a", act(out[:, 16 * a:16 * b], win[:].indirect(lst[:, a:b])), reads, keys)

    def lin(groups, reads, key, begin=True, end=True):
        calls = []
        for out, terms in groups:
            for i, (W, x) in enumerate(terms):
                a, z = begin and i == 0, end and i == len(terms) - 1
                calls.append(lambda out=out, W=W, x=x, a=a, z=z: g.tensor.matmul(out, W, x, a, z))
        batch("p", calls, reads + ["ident"], key)

    Ip, Jn, Jp = T.Ip[:], T.Jn[:], T.Jp[:]

    def role(t, side, j):
        return T["N%d" % t][:, :, side, j::2] if t else T.N0[:, :, side, j]

    def brole(t, side, j):
        hi = 2 ** (6 - t)
        return T["B%d" % t][:, j * hi:(j + 1) * hi, side, :] if t else T.B0[:, j * hi:(j + 1) * hi, side]

    def blk(side, j):
        return 64 * (2 * j + side)

    first_mm = [True]

    def sums(items, reads, last):
        for i, (P, W, rhs) in enumerate(items):
            st, fin = first_mm[0], last and i == len(items) - 1
            first_mm[0] = fin
            op("p", lambda: g.tensor.matmul(T.D[:, 0:64], W[:, 16 - P:144 - P], rhs, st, fin),
               reads + ["Wp", "Wn"], ["D"] if st else [], [] if st else ["D"])

    def entry_list(t, reads):
        N, calls = T["N%d" % t], []
        for r in range(8):
            c7, r4, tb = r >> 2, (r >> 1) & 1, r & 1
            if t <= 3:
                sp = 2 ** (4 - t)
                h0 = (2 * c7 + r4) * sp
                src = N[:, h0 + tb:h0 + sp:2, :, :] if t < 3 else N[:, h0 + tb, :, :]
            else:
                src = N[:, 2 * c7 + tb, r4, :]
            calls.append(code(T.o16[:, r:256:8], src) if t else cp(T.Oout[:, r:256:8], src))
        batch("v", calls, reads, "o16")

    done = [0, 0, 0]

    def window(w, upto, q="a"):
        Vw = T["V%d" % w]
        for u in range(done[w], upto):
            run, step = slice(256 * u, 256 * u + 256), slice(u, 4096, 16)
            out, in_ = ((run, run), (step, run), (run, step))[w]
            if q == "a":
                call = act(Vw[:, out], T.xs[:, in_])
            else:
                call = lambda: g.affine_select(Vw[:, out], T.xs[:, in_], [[0, 256]], A.is_ge, 0.0, 0, 0)
            wr.setdefault("V%d" % w, {})
            op(q, call, ["xs"], [], ["V%d" % w])
        done[w] = upto

    def rows(w, ps):
        for p in ps:
            dma(T["X%d%d" % (w, p)][:], T["V%d" % w][p:128:16, :], ["V%d" % w], ["X%d%d" % (w, p)])

    def ride(w, p, tile):
        Vn = "V%d" % w
        dma(T[Vn][p:128:16, :], T[tile][:], [tile, Vn, "X%d%d" % (w, p)], ["%s.%d" % (Vn, p)])

    small = dict(allow_small_or_imprecise_dtypes=True)
    dma(T.G[:], T.o[:], [], ["G"])
    op("g", lambda: g.iota(T.ZD[:, 0:256], [[16, 128], [2048, 2]], int(LIFT), 0, **small), [], ["ZD0"])
    op("g", lambda: g.iota(T.pi[:], [[1, 1]], 0, 1), [], ["pi"])
    op("g", lambda: g.iota(T.dg[:], [[1, 128]], 0, -1, **small), [], ["dg"])
    op("g", lambda: g.iota(T.ZD[:, 256 * NB:256 * (NB + NG)], [[1, NG], [16, 128], [2048, 2]], int(LIFT) + NB, 0, **small),
       [], ["ZDg"])
    op("v", lambda: V.memset(T.zero[:], 0.0), [], ["zero"])
    dma(T.Z[0:128:16, :], T.zero[:], ["zero"], ["Z.v"])
    dma(T.GO[0:128:16, :], T.zero[:], ["zero"], ["GO.a"])
    dma(T.xs[:], T.x[:], [], ["xs"])
    dma(T.X00[:], T.x[0:128:16, :], [], ["X00"])
    dma(T.X01[:], T.x[1:128:16, :], [], ["X01"])
    batch("a", [act(T.ZD[:, 256 * P:256 * P + 256], T.ZD[:, 0:256], P, ACT.Silu) for P in range(NB + NG, 16)],
          ["ZD0"], "ZDa")
    op("v", lambda: V.memset(T.Wp[:], 0.0), [], ["Wp"])
    op("v", lambda: V.memset(T.Wn[:], 0.0), [], ["Wn"])
    op("v", lambda: V.memset(T.Wp[:, 0:144:16], 1.0), [], ["Wp"])
    op("v", lambda: V.memset(T.Wn[:, 0:144:16], -1.0), [], ["Wn"])
    op("v", ts(T.pj[:], T.pi[:], 4, 1, A.logical_shift_right, A.bitwise_and), ["pi"], ["pj"])
    op("v", ts(T.pk[:], T.pi[:], 15, None, A.bitwise_and), ["pi"], ["pk"])
    op("v", cp(T.m1[:], T.pj[:]), ["pj"], ["m1"])
    op("v", ts(T.m0[:], T.pj[:], -1.0, 1.0, A.mult, A.add), ["pj"], ["m0"])
    op("v", ts(T.pc[:], T.pk[:], 4096.0 * OFF - MID, None, A.add), ["pk"], ["pc"])
    batch("v", [ts(T.Sel[:, 2 * q + c, :], T.dg[:], 16.0 * (c - q), (T.m0, T.m1)[q][:], A.is_equal, A.mult)
                for q in (0, 1) for c in (0, 1)], ["dg", "m0", "m1"], "ident")
    op("v", cp(T.G16[:], T.G[:]), ["G"], ["G16"])
    for a, b, key in ((NB + NG, 16, "ZDa"), (NB, NB + NG, "ZDg")):
        op("a", lambda: S.activation(T.GO[:].indirect(T.G16[:, 16 * a:16 * b]), T.ZD[:, 256 * a:256 * b], ACT.Silu),
           ["G16", key], ["GO.a"])
    batch("v", [cp(T.Gr[:, 32 * (u & 7) + 16 * (u >> 3):32 * (u & 7) + 16 * (u >> 3) + 16], T.G[:, u:256:16])
                for u in range(16)], ["G"], "Gr")
    batch("v", [(lambda u=u: V.transpose(T.Gt[:, u, :], T.Gr[:, 32 * u:32 * u + 32])) for u in range(8)], ["Gr"], "Gt")
    lin([(T.Pa[:, 128 * q:128 * q + 128], [(T.Sel[:, 2 * q + c, :], T.Gt[:, :, 16 * c:16 * c + 16]) for c in (0, 1)])
         for q in (0, 1)], ["Gt"], "Pa")
    for P in range(NB):
        op("v", ts(T.Z[:].indirect(T.G16[:, 16 * P:16 * P + 16]), T.ZD[:, 0:256], 1.0, float(P), A.mult, A.add),
           ["G16", "ZD0"], ["Z.v"])
        if P == NE - 1:
            op("v", cp(T.N0[:], T.Pa[:, 0:256]), ["Pa"], ["N"])
            entry_list(0, ["N"])
            send([T.Oout], T.Oin, ["oin", "oin"], ["o16"])
            op("g", lambda: g.iota(T.ZD[:, 256:256 * NB], [[0, 256 * (NB - 1)]], 0, 0, **small), [], ["ZDf"])
            op("g", lambda: g.iota(T.c16[:], [[16, 256]], 0, 0, **small), [], ["c16"])
    dma(T.Tv[:], T.Z[0:128:16, :], ["Z.v"], ["Tv"])
    dma(T.Ta[:], T.GO[0:128:16, :], ["GO.a"], ["Ta"])
    rd["Z.a"], rd["GO.v"] = dict(rd["Z.v"]), dict(rd["GO.a"])
    batch("v", [cp(T.H16[:, blk(sd, j):blk(sd, j) + 64], T.Pa[:, 2 * sd + j:256:4]) for sd in (1, 0) for j in (0, 1)],
          ["Pa"], "H16")

    zk = ["Z.v", "Z.a"]
    gk = ["GO.v", "GO.a"]
    j0, j1 = slice(0, 64), slice(64, 128)
    for t in range(RO + 1):
        w, iex, iin = t % 3, "Iex%d" % t, "Iin%d" % t
        if t > 0:
            Vn = "V%d" % ((t - 1) % 3) if t < RO else "CW"
            wk = [Vn] + ["%s.%d" % (Vn, p) for p in range(3)]
            b0, b1 = "Bin%d_0" % (t - 1), "Bin%d_1" % (t - 1)
            Bin = T["Bin%d" % (t - 1)]
            mid, cut = (GL, ZC) if t >= RO - 1 else (GV, 256)
            gv(T.Z, T[Vn], Bin, 0, mid, wk + [b0] + ([b1] if mid > 128 else []), ["Z.v"])
            ga(T.Z, T[Vn], Bin, mid, cut, wk + [b1] + ([b0] if mid < 128 else []), ["Z.a"])
            if t > 1:
                op("a", act(T.rH[:], T.Hf[:]), ["Hf"], ["rH"])
            if cut < 256:
                op("a", act(T.Z[:, 16 * cut:4096], T[Vn][:].indirect(Bin[:, cut:256])), wk + [b1], [], ["Z.a"])
            if t == RO:
                lin([(T.Ph[:, 0:256], [(Ip, T.Hf[:]), (Jn, T.rH[:])])], ["Hf", "rH"], "Ph")
                op("v", code(T.H16[:], T.Ph[:, 0:256]), ["Ph"], ["H16"])
                gv(T.GO, T.Z, T.H16, 0, 128, zk + ["H16"], ["GO.v"])
                ga(T.GO, T.Z, T.H16, 128, 256, zk + ["H16"], ["GO.a"])
                dma(T.yo[:], T.GO[0:128:16, :], gk, [])
                break
            if t > 1:
                lin([(T.Ph[:, 64 * z:64 * z + 64], [(Ip, T.Hf[:, :, z, :]), (Jn, T.rH[:, :, z, :])]) for z in range(4)],
                    ["Hf", "rH"], "Ph")
            if t == 2:
                rows(2, (0, 1))
            if t < RO - 1:
                lin([(T.Pe[:, 0:256], [(Ip if w else Jp, T["X%d1" % w][:])])], ["X%d1" % w], "Pe", end=False)
            if t == RO - 2:
                lin([(T.Pk[:, 0:256], [(Ip, T.X12[:])])], ["X12"], "Pk", end=False)
            if t < RO - 1:
                lk = "L16" if t > 1 else "Iin0"
                gv(T.GO, T.Z, T[lk], 0, IV, zk + [lk], ["GO.v"])
                ga(T.GO, T.Z, T[lk], IV, 256, zk + [lk], ["GO.a"])
                dma(T[iex][:], T.GO[1:128:16, :], gk, ["Iex"])
            else:
                dma(T[iex][:], T.Z[1:128:16, :], zk, ["Iex"])
            send([T[iex]], T[iin], ["i%d" % t] * 2, ["Iex"])
            if t == 1:
                window(2, G2 + 5, "g")
            if t > 1:
                calls = [code(T.H16[:, z:256:4], T.Ph[:, 64 * z:64 * z + 64]) for z in range(4)]
            else:
                calls = [ts(T.H16[:, z:256:4], T.Hin[:, :, z, :], 0.25 - LIFT, None, A.add) for z in range(4)]
            batch("v", calls, ["Ph" if t > 1 else "Hin"], "H16")
            hk = zk + ["H16"]

            def piece(eng, side, j, h, key):
                a = blk(side, j) + 32 * h
                eng(T.AB, T.Z, T.H16, a, a + (32 if side else 64), hk, [key])

            def fold(out, p, side, j, key):
                c = 16 * blk(side, j)
                dma(out, T.AB[p:128:16, c:c + 1024], ["b%d0" % j, "b%d1" % j] if side else ["a%dr" % j], [key])

            def fused(M, j, jb, p0, p1, last=False):
                key = "%s.%d.%d" % (M, j, p0)
                lo, a, b = 1024 * j, blk(0, j), 16 * blk(1, jb)
                op("v", tt(T[M][:, lo + 64 * p0:lo + 64 * p1], T.Z[:].indirect(T.H16[:, a + 4 * p0:a + 4 * p1]),
                           T.AB[:, b + 64 * p0:b + 64 * p1], A.max), hk + ["b%d%d" % (jb, p0 // 8)], [key])
                sums([(P, T.Wp if M == "M1" else T.Wn, T[M][:, lo + 64 * P:lo + 64 * P + 64]) for P in range(p0, p1)],
                     [key], last)

            def whole(r, E, j):
                op("a", act(T[r][:, (j0, j1)[j]], T[E][:, (j0, j1)[j]]), ["%s%d" % (E, j)], ["%s%d" % (r, j)])

            kk = []

            def second(sd, j):
                if t == RO - 1:
                    kk.append("K%d%d" % (sd, j))
                    fold(T.et[:, blk(sd, j):blk(sd, j) + 64], 2, sd, j, kk[-1])

            piece(gv, 1, 0, 0, "b00")
            piece(ga, 1, 1, 0, "b10")
            piece(ga, 1, 0, 1, "b01")
            fold(T.Eb[:, j0], 0, 1, 0, "Eb0")
            piece(ga, 1, 1, 1, "b11")
            fold(T.Eb[:, j1], 0, 1, 1, "Eb1")
            piece(ga, 0, 0, 0, "a0r")
            fold(T.Ea[:, j0], 0, 0, 0, "Ea0")
            second(1, 0)
            second(1, 1)
            piece(ga, 0, 1, 0, "a1r")
            fold(T.Ea[:, j1], 0, 0, 1, "Ea1")
            second(0, 0)
            second(0, 1)
            whole("rb", "Eb", 1)
            whole("rb", "Eb", 0)
            whole("ra", "Ea", 0)
            whole("ra", "Ea", 1)
            fused("M1", 0, 0, 0, 8)
            fused("M2", 1, 0, 0, 8)
            fused("M1", 1, 1, 0, 8)
            fused("M2", 0, 1, 0, 8)
            fused("M1", 0, 0, 8, 16)
            fused("M2", 1, 0, 8, 16)
            if PBE:
                lin([(T.Pb[:, j0], [(Ip, T.Eb[:, j1]), (Jn, T.rb[:, j1])])], ["Eb1", "rb1"], "Pb")
            fused("M1", 1, 1, 8, 16)
            if not PBE:
                lin([(T.Pb[:, j0], [(Ip, T.Eb[:, j1]), (Jn, T.rb[:, j1])])], ["Eb1", "rb1"], "Pb")
            fused("M2", 0, 1, 8, 13)
            fused("M2", 0, 1, 13, 16, True)
            lin([(T.Pa[:, j0], [(Ip, T.Ea[:, j1]), (Jn, T.ra[:, j1])])], ["Ea1", "ra1"], "Pa")
            a0, b0 = (role(t, 0, 0), role(t, 1, 0)) if t < RO - 1 else (T.a0[:], T.b0[:])
            op("v", tt(b0, T.Eb[:, j0], T.rb[:, j0], A.subtract), ["Eb0", "rb0"], ["b0"])
            op("v", tt(a0, T.Ea[:, j0], T.ra[:, j0], A.subtract), ["Ea0", "ra0"], ["a0"])
            op("v", tt(T.db[:], T.Pb[:, j0], b0, A.subtract), ["Pb", "b0"], ["db"])
            dma(T.ZD[0:128:16, :], T[iin][:], [iin], ["ZD0", "ZDg"])
            if t < RO - 1:
                op("a", act(T.rE[:], T[iex][:]), ["Iex"], ["rE"])
                lin([(T.Pe[:, 0:256], [(Ip, T[iex][:]), (Jn, T.rE[:])])], ["Iex", "rE"], "Pe", begin=False)
            else:
                op("a", act(T.rE[:], T.et[:]), kk, ["rE"])
                lin([(T.Pe[:, 0:256], [(Ip, T.et[:]), (Jn, T.rE[:])])], kk + ["rE"], "Pe")
            val = lambda sd, j: ((a0, T.Pa[:, j0]), (b0, T.Pb[:, j0]))[sd][j]
            ka, kb = ["Pa", "a0"], ["Pb", "b0"]
        else:
            for eng, a, b in (("v", 0, B0), ("a", B0, 128)):
                for j in (0, 1):
                    lo, hi = max(a, 64 * j), min(b, 64 * j + 64)
                    if lo < hi:
                        c = blk(1, j) - 64 * j
                        src, out = T.xs[:].indirect(T.H16[:, c + lo:c + hi]), T.bb[:, 16 * lo:16 * hi]
                        op(eng, cp(out, src) if eng == "v" else act(out, src), ["xs", "H16"], ["bb%s%d" % (eng, j)])
            window(0, 1)
            window(0, 1 + G0, "g")
            window(0, 16)
            window(1, W1)
            for M, j, jb in (("M1", 0, 0), ("M2", 1, 0), ("M1", 1, 1), ("M2", 0, 1)):
                keys = ["%s.%d.%d" % (M, j, p0) for p0 in (0, 8, 13)]
                op("v", tt(T[M][:, 1024 * j:1024 * j + 1024], T.xs[:].indirect(T.H16[:, blk(0, j):blk(0, j) + 64]),
                           T.bb[:, 1024 * jb:1024 * jb + 1024], A.max), ["xs", "H16", "bbv%d" % jb, "bba%d" % jb], keys)
                sums([(P, T.Wp if M == "M1" else T.Wn, T[M][:, 1024 * j + P:1024 * j + 1024:16]) for P in range(16)],
                     keys, (M, j) == ("M2", 0))
            op("v", tt(T.Gr[:], T.Tv[:], T.Ta[:], A.add), ["Tv", "Ta"], ["Gr"])
            dma(T.ZD[0:128:16, :], T.Gr[:], ["Gr"], ["ZD0", "ZDg", "ZDa", "ZDf"])
            op("v", tt(T.db[:], role(0, 1, 1), role(0, 1, 0), A.subtract), ["N"], ["db"])
            op("v", tt(T.da[:], role(0, 0, 1), role(0, 0, 0), A.subtract), ["N"], ["da"])
            op("v", ts(T.cod[:], T.c16[:], T.pc[:], 1.0 / 4096.0, A.add, A.mult), ["c16", "pc"], ["cod"])
            val = lambda sd, j: role(0, sd, j)
            ka, kb = ["N"], ["N"]
        s = T.Pc[:, j0]
        op("v", ts(s, T.D[:, j0], 0.0, None, A.is_gt), ["D"], ["s"])
        op("v", tt(T.eb[:], T.db[:], s, A.mult), ["db", "s"], ["eb"])
        if t:
            op("v", tt(T.da[:], val(0, 1), val(0, 0), A.subtract), ka, ["da"])
        op("v", tt(brole(t, 0, 0), val(1, 0), T.eb[:], A.add), kb + ["eb"], ["Bb"])
        op("v", tt(T.ea[:], T.da[:], s, A.mult), ["da", "s"], ["ea"])
        op("v", tt(brole(t, 0, 1), val(1, 1), T.eb[:], A.subtract), kb + ["eb"], [], ["Bb"])
        batch("v", [tt(brole(t, 1, 0), val(0, 1), T.ea[:], A.subtract), tt(brole(t, 1, 1), val(0, 0), T.ea[:], A.add)],
              ka + ["ea"], "Ba")
        Bt, Bo = T["B%d" % t][:], T["Bout%d" % t][:]
        op("v", code(Bo, Bt) if t else cp(Bo, Bt), ["Ba", "Bb"], ["Bout"])
        send([T["Bout%d" % t]], T["Bin%d" % t], ["b%d_0" % t, "b%d_1" % t], ["Bout"])
        N = T["N%d" % t]
        if t == RO - 1:
            batch("v", [code(role(t, sd, j), T.Pe[:, blk(sd, j):blk(sd, j) + 64]) for sd in (0, 1) for j in (0, 1)],
                  ["Pe"], "N")
            op("v", cp(T.o16[:], N[:]), ["N"], ["o16"])
        else:
            if t:
                batch("a", [act(role(t, sd, 1), val(sd, 1)) for sd in (1, 0)], ka + kb + ["Ba", "Bb"], "N")
                entry_list(t, ["N"] + ka + kb)
        if t == 0:
            op("v", ts(T.tk[:], T.Gr[:], 2048.25 - LIFT, None, A.add), ["Gr"], ["tk"])
            op("v", tt(T.st[:], T.cod[:], T.X00[:], A.add), ["cod", "X00"], ["st"])
            ride(0, 0, "st")
            op("v", ts(T.ti[:], T.tk[:], 4095, None, A.bitwise_and), ["tk"], ["ti"])
            op("v", ts(T.et[:], T.tk[:], 4096.0 * OFF - MID - 2048.0, 1.0 / 4096.0, A.add, A.mult), ["tk"], ["et"])
            op("v", cp(T.G16[:], T.ti[:]), ["ti"], ["G16"])
            send([T.G16], T.Iin0, ["i0", "i0"], ["G16"])
            op("v", tt(T.emb[:], T.et[:], T.X01[:], A.add), ["et", "X01"], ["emb"])
            ride(0, 1, "emb")
            gv(T.GO, T.ZD, T.Oin, 0, HV0, ["ZD0", "Oin"], ["GO.v"])
            ga(T.GO, T.ZD, T.Oin, HV0, 256, ["ZD0", "Oin"], ["GO.a"])
            batch("v", [ts(W, T.dg[:], 0.0, sg, A.is_equal, A.mult) for W, sg in ((Ip, 1.0), (Jn, -1.0), (Jp, 1.0))],
                  ["dg"], "ident")
            dma(T.Hv[:], T.GO[0:128:16, :], gk, ["Hv"])
            window(1, W1 + G1, "g")
            send([T.Hv], T.Hin, ["hin", "hin"], ["Hv"])
            window(1, W1 + G1 + W2)
            window(1, 16, "g")
            rows(1, (0, 1))
            window(2, G2, "g")
            continue
        if t == 1:
            window(2, 16, "g")
        if t == 2:
            op("g", lambda: g.iota(T.CW[:], [[1, 16], [16, 256]], 0, 0, **small), [], ["CW"])
        if t < RO - 1:
            op("a", act(T.emb[:], T.Pe[:, 0:256], OFF), ["Pe"], ["emb"])
            ride(w, 1, "emb")
        if t < 3:
            op("v", tt(T.st[:], T.cod[:], T["X%d0" % w][:], A.add), ["cod", "X%d0" % w], ["st"])
            ride(w, 0, "st")
        if t < RO - 2:
            op("a", act(T.rL[:], T[iin][:], 0.5), [iin], ["rL"])
            lin([(T.Pl[:, 0:256], [(Ip, T[iin][:]), (Jn, T.rL[:])])], [iin, "rL"], "Pl")
        elif t == RO - 2:
            op("a", act(T.rL[:], T.Kin[:], 0.5), ["Kin"], ["rL"])
            lin([(T.Pk[:, 0:256], [(Ip, T.Kin[:]), (Jn, T.rL[:])])], ["Kin", "rL"], "Pk", begin=False)
        if t == 2:
            rows(1, (2,))
        hv = HV1 if t == 1 else HV
        cut = hv + 56 if t == RO - 2 else 256
        gv(T.GO, T.ZD, T.o16, 0, hv, ["ZD0", "o16"], ["GO.v"])
        ga(T.GO, T.ZD, T.o16, hv, cut, ["ZD0", "o16"], ["GO.a"])
        if t == RO - 2:
            op("a", act(T.st[:], T.Pk[:, 0:256], OFF + 0.5), ["Pk"], ["st"])
            ride(w, 2, "st")
            op("a", act(T.GO[:, 16 * cut:4096], T.ZD[:].indirect(T.o16[:, cut:256])), ["ZD0", "o16"], [], ["GO.a"])
        dma(T.Hf[:], T.GO[0:128:16, :], gk, ["Hf"])
        if t < RO - 2:
            op("v", code(T.L16[:], T.Pl[:, 0:256], 2048.0), ["Pl"], ["L16"])
    need("g", top)
